import numpy as np
import ml_dtypes


def mxq(x, axis, fmt="e4m3"):
    dtype, down = {"e4m3": (ml_dtypes.float8_e4m3fn, 7), "e5m2": (ml_dtypes.float8_e5m2, 14)}[fmt]
    v = np.moveaxis(np.asarray(x, np.float32).astype(ml_dtypes.bfloat16).astype(np.float64), axis, -1)
    blocks = v.reshape(v.shape[:-1] + (-1, 32))
    amax = np.abs(blocks).max(-1, keepdims=True)
    byte = np.maximum(np.where(amax > 0, np.frexp(amax)[1] - 1 + 127, 0) - down, 1)
    scale = np.exp2(byte - 127.0)
    codes = (blocks / scale).astype(np.float32).astype(dtype).astype(np.float64)
    return np.moveaxis((codes * scale).reshape(v.shape), -1, axis)


WIDE = False


def mx_kscale(k):
    if not WIDE:
        return np.ones(k)
    levels = np.array([10, -10, 5, -5, 0])
    if k % 512:
        return np.exp2(np.random.permutation(np.resize(levels, k // 32))).repeat(32)
    a = np.empty((k // 512, 16))
    for p in range(k // 512):
        a[p, :8] = np.random.permutation(np.resize(levels, 8))
        for g in range(8):
            far = levels[np.abs(levels - a[p, g]) >= 10]
            a[p, g + 8] = far[np.random.randint(len(far))]
    return np.exp2(a.ravel()).repeat(32)


BF16 = ml_dtypes.bfloat16


def bf(x):
    return np.asarray(x, np.float32).astype(BF16)


def f64(x):
    return np.asarray(x).astype(np.float64)


E2M1 = np.array([0.0, 0.5, 1.0, 1.5, 2.0, 3.0, 4.0, 6.0, -0.0, -0.5, -1.0, -1.5, -2.0, -3.0, -4.0, -6.0])


def pack_weight(w, fmt):
    k, n = w.shape
    w = f64(bf(w)).reshape(k // 32, 32, n)
    amax = np.abs(w).max(1)
    if fmt == "e4m3":
        byte = np.frexp(amax)[1] - 1 + 127 - 7
    else:
        mant, ex = np.frexp(amax / 6.0)
        byte = np.where(mant > 0.5, ex, ex - 1) + 127
    byte = np.clip(np.where(amax > 0, byte, 1), 1, 254)
    scaled = (w * np.exp2(127.0 - byte)[:, None, :]).reshape(k, n).astype(np.float32)
    by_word = np.ascontiguousarray(scaled.reshape(k // 512, 128, 4, n).transpose(0, 1, 3, 2))
    if fmt == "e4m3":
        words = by_word.astype(ml_dtypes.float8_e4m3fn).view(np.uint8)
    else:
        c = by_word.astype(ml_dtypes.float4_e2m1fn).view(np.uint8) & 0xF
        words = c[..., 0::2] | (c[..., 1::2] << 4)
    return np.ascontiguousarray(words), np.ascontiguousarray(byte.astype(np.uint8).reshape(k // 512, 16, n))


def unpack_weight(words, scales, fmt):
    g, p, n, _ = words.shape
    if fmt == "e4m3":
        vals = np.ascontiguousarray(words).view(ml_dtypes.float8_e4m3fn).astype(np.float64)
    else:
        nib = np.empty((g, p, n, 4), np.uint8)
        nib[..., 0::2] = words & 0xF
        nib[..., 1::2] = words >> 4
        vals = E2M1[nib]
    vals = vals * np.repeat(np.exp2(scales.astype(np.float64) - 127.0), 8, axis=1)[..., None]
    return vals.transpose(0, 1, 3, 2).reshape(g * 512, n)
def pack4(w):
    words, scales = pack_weight(w, "e2m1")
    return words.reshape(words.shape[0], 128, -1), scales


def unpack4(words, scales):
    return unpack_weight(words.reshape(words.shape[0], 128, -1, 2), scales, "e2m1")


M, D, P, R, B = 1024, 1024, 2048, 1024, 512


def setup_inputs():
    s = mx_kscale(D)
    r = mx_kscale(R)
    t = mx_kscale(P)
    amp = np.random.uniform(0.4, 1.2, (P, 1))
    points = amp * np.random.standard_normal((P, D)) / np.sqrt(D)
    energy = 0.5 * (points ** 2).sum(1)
    u = np.random.standard_normal((R, P)) * r[:, None] / t
    v = np.random.standard_normal((R, B)) / np.sqrt(R) * P ** -0.25 / r[:, None]
    u_words, u_scales = pack4(u)
    v_words, v_scales = pack4(v)
    return {"y": bf(np.random.standard_normal((M, D)) * s),
            "points": bf(points / s),
            "energy": bf(energy),
            "prior": bf(np.random.uniform(0.2, 0.6, P) * t),
            "u_words": u_words, "u_scales": u_scales,
            "v_words": v_words, "v_scales": v_scales}


def reference(y, points, energy, prior, u_words, u_scales, v_words, v_scales):
    ip = mxq(f64(y), 1, "e4m3") @ mxq(f64(points), 1, "e4m3").T
    like = np.exp(ip - f64(energy)) * f64(prior)
    labels = unpack4(u_words, u_scales).T @ unpack4(v_words, v_scales)
    return mxq(like, 1, "e4m3") @ mxq(labels, 0, "e4m3")

@@ -1,0 +1,375 @@
+from contextlib import ExitStack
+
+import concourse.mybir as mybir
+from concourse.masks import make_identity
+
+M, D, NPTS, R, B = 1024, 1024, 2048, 1024, 512
+FLOPS = 2 * M * D * NPTS + 2 * R * NPTS * B + 2 * M * NPTS * B
+
+F32 = mybir.dt.float32
+BF16 = mybir.dt.bfloat16
+I32 = mybir.dt.int32
+U32 = mybir.dt.uint32
+U8 = mybir.dt.uint8
+FP8X4 = mybir.dt.float8_e4m3fn_x4
+FP4X4 = mybir.dt.float4_e2m1fn_x4
+ALU = mybir.AluOpType
+ACT = mybir.ActivationFunctionType
+
+P = 128
+BANKS = 8
+SORT_LEAD = 3
+USORT_LEAD = 3
+QUANT_LAG = 2
+WEAVE_LAG = (10, 1)
+LAB_LAG = 1
+WARM = 3
+WARM2 = 6
+LEVAC_LAG = 1
+WQ_LAG = 2
+SORT_MIN = {}
+HEAD = "L00 L01 L02 L03 Ty00 L10 Ty01 L11 Tx00 L12 Tx01 L13 Tx10"
+SLOT = "T T I I L I I L"
+TAIL = "S004 S104 S204 S304 S403 S503 S434 S534 S604 S70401 S70412"
+P2 = {}
+LOADS = "v u0 us vs y00 u1 y01 x00 x01 x10 u2 x11 u3 x20 x21 x30 x31 y10 y11"
+SORT_ON_S = ("y00", "y01")
+RES_V = (1, 3, 5, 7)
+
+
+def unit_order():
+    def parse(w):
+        if w[0] == "T":
+            return ("T", w[1], int(w[2]), int(w[3]))
+        return (w[0],) + tuple(int(c) for c in w[1:])
+
+    u = [("C",)] + [parse(w) for w in HEAD.split()]
+    turns = [("T", "y", 0, 0), ("T", "y", 0, 1)] + [("T", "x", G, a) for G in range(4) for a in range(2)] + [("T", "y", 1, 0), ("T", "y", 1, 1)]
+    turns = [t for t in turns if t not in u]
+    labs = [("L", G, c) for G in range(4) for c in range(4)]
+    labs = [t for t in labs if t not in u]
+    ips = [("I", 0, G, t) for G in range(4) for t in range(4)]
+    for G in range(4):
+        for w in SLOT.split():
+            q = {"I": ips, "T": turns, "L": labs}[w]
+            if q:
+                u.append(q[0])
+                q.remove(q[0])
+    for G in range(4):
+        for t in range(4):
+            u.append(("I", 1, G, t))
+            if labs:
+                u.append(labs[0])
+                labs.remove(labs[0])
+            if (G, t) in P2:
+                u.append(parse(P2[(G, t)]))
+    u.extend([parse(w) for w in TAIL.split()])
+    return u
+
+
+def tile_soft_demapper_label_sums_s12_kernel(
+    tc, y, points, energy, prior, u_words, u_scales, v_words, v_scales, out
+):
+    nc = tc.nc
+    with ExitStack() as ctx:
+        keep = ctx.enter_context(tc.tile_pool(name="keep", bufs=1))
+        work = ctx.enter_context(tc.tile_pool(name="work", bufs=3))
+        psum = ctx.enter_context(tc.psum_pool(name="psum", bufs=1))
+        ctx.enter_context(tc.manual_schedule())
+
+        def kept(name, shape, dtype):
+            return keep.tile(shape, dtype, name=name, align_bytes=64)
+
+        banks = []
+
+        def new_bank():
+            bank = psum.tile([P, 512], F32, name="bank%d" % len(banks), tag="bank%d" % (len(banks) % BANKS))
+            banks.append(bank)
+            return bank
+
+        def mx_operand(name):
+            return kept(name + "_codes", [P, 512], U32), kept(name + "_scales", [P, 512], U8)
+
+        c_raw = kept("c_raw", [8, 512], BF16)
+        nc.scalar.dma_start(out=c_raw[4:8, :], in_=prior.rearrange("(g c) -> g c", g=4))
+        nc.scalar.dma_start(out=c_raw[0:4, :], in_=energy.rearrange("(g c) -> g c", g=4))
+        probe = kept("probe", [P, 2], F32)
+        nc.vector.memset(probe[:, 0:1], 1.0)
+        nc.scalar.activation(out=probe[:, 1:2], in_=probe[:, 0:1], func=ACT.Ln)
+        us_raw = kept("us_raw", [P, 2 * NPTS], U8)
+        vs = kept("vs", [P, 2 * B], U8)
+        nc.vector.memset(us_raw[:].bitcast(I32), 0)
+        nc.vector.memset(vs[:].bitcast(I32), 0)
+        c_sorted = kept("c_sorted", [P, 512], F32)
+
+        ident = kept("ident", [P, P], F32)
+        make_identity(nc, ident[:])
+
+        raw = {}
+
+        def load_rows(src, s, pair):
+            rows = (y if src == "y" else points)[512 * s + 256 * pair : 512 * s + 256 * (pair + 1), :]
+            tile = kept("raw_%s%d%d" % (src, s, pair), [P, 2, D], BF16)
+            nc.sync.dma_start(out=tile[:], in_=rows.rearrange("(a p) d -> p a d", p=P))
+            raw[(src, s, pair)] = tile
+
+        u_raw = {}
+
+        def load_u(G):
+            tile = kept("u_raw%d" % G, [P, 2, 256], I32)
+            nc.sync.dma_start(out=tile[:], in_=u_words.bitcast(I32).rearrange("g p w -> p g w")[:, :, 256 * G : 256 * (G + 1)])
+            u_raw[G] = tile
+
+        def load_scales(plane, src):
+            rows = src.bitcast(I32).rearrange("g (quad r) w -> r quad g w", r=4)
+            for r in range(4):
+                nc.sync.dma_start(out=plane[r:P:32, :].bitcast(I32).rearrange("p (g w) -> p g w", g=2), in_=rows[r])
+
+        v_codes = kept("v_codes", [P, 2 * 2 * B], U8)
+        for w in LOADS.split():
+            if w == "v":
+                nc.sync.dma_start(out=v_codes[:].bitcast(I32).rearrange("p (g w) -> p g w", g=2), in_=v_words.bitcast(I32).rearrange("g p w -> p g w"))
+            elif w == "us":
+                load_scales(us_raw, u_scales)
+            elif w == "vs":
+                load_scales(vs, v_scales)
+            elif w[0] == "u":
+                load_u(int(w[1]))
+            else:
+                load_rows(w[0], int(w[1]), int(w[2]))
+
+        nc.gpsimd.memset(c_sorted[:], 0.0)
+        if WARM:
+            warm_bf = kept("warm_bf", [P, 1024], BF16)
+            nc.vector.memset(warm_bf[:].bitcast(I32), 0)
+            warm_codes = kept("warm_codes", [P, 256], U32)
+            warm_scales = kept("warm_scales", [P, 256], U8)
+            nc.vector.quantize_mx(out=warm_codes[:].bitcast(FP8X4), scales=warm_scales[:], in_=warm_bf[:])
+
+        srt = {}
+
+        def sort_words(src, s, pair):
+            tile = work.tile([P, 2, 2 * D // 2], BF16, name="srt", tag="srt", bufs=4, align_bytes=64)
+            copy = nc.scalar.copy if "%s%d%d" % (src, s, pair) in SORT_ON_S else nc.vector.tensor_copy
+            copy(
+                out=tile[:].rearrange("p u (b e) -> p u b e", e=16),
+                in_=raw[(src, s, pair)][:].rearrange("p a (b u e) -> p u (a b) e", u=2, e=16),
+            )
+            srt[(src, s, pair)] = tile
+
+        u_codes = {}
+        u_sc = {}
+
+        def sort_u(G):
+            codes = kept("u_codes%d" % G, [P, 2 * 1024], U8)
+            nc.vector.tensor_copy(
+                out=codes[:].bitcast(I32).rearrange("p (g t q w) -> p g t q w", g=2, t=4, w=4),
+                in_=u_raw[G][:].rearrange("p g (q t w) -> p g t q w", t=4, w=4),
+            )
+            u_codes[G] = codes
+
+        def sort_us(G):
+            sc = kept("u_sc%d" % G, [P, 2 * 512], U8)
+            nc.vector.tensor_copy(
+                out=sc[:].bitcast(I32).rearrange("p (g t q w) -> p g t q w", g=2, t=4, w=2),
+                in_=us_raw[:].bitcast(I32).rearrange("p (g G q t w) -> p G g t q w", g=2, G=4, t=4, w=2)[:, G],
+            )
+            u_sc[G] = sc
+
+        def quantise(tile, operand):
+            nc.vector.quantize_mx(out=operand[0][:].bitcast(FP8X4), scales=operand[1][:], in_=tile[:])
+
+        woven = {}
+        like_bf = {}
+        operands = {}
+
+        def quantise_like(key):
+            quantise(woven[key], operands[("like",) + key])
+
+        def weave(key):
+            dst = work.tile([P, 2048], BF16, name="woven", tag="woven", bufs=2, align_bytes=64)
+            woven[key] = dst
+            src = like_bf[key]
+            nc.vector.tensor_copy(
+                out=dst[:].rearrange("p (c i t) -> p c t i", i=4, t=4),
+                in_=src[:].rearrange("p t (c i) -> p c t i", i=4),
+            )
+
+        consts = kept("consts", [P, 8, 4], F32)
+        sign = kept("sign", [P, 16], F32)
+        half_sign = kept("half_sign", [P, 16], F32)
+        neg = kept("neg", [P, 16], F32)
+        mag = kept("mag", [P, 16], F32)
+        parts = kept("parts", [P, 3, 16], F32)
+        logs = kept("logs", [P, 3, 16], F32)
+        log_mag = kept("log_mag", [P, 16], F32)
+        bias = kept("bias", [P, 16], F32)
+        e_cols = consts[:, 0:4, :].rearrange("p g t -> p (g t)")
+        p_cols = consts[:, 4:8, :].rearrange("p g t -> p (g t)")
+
+        def sort_consts():
+            nc.vector.tensor_copy(
+                out=c_sorted[0:8, :].rearrange("p (t q r) -> p t q r", t=4, r=8),
+                in_=c_raw[:].rearrange("p (q t r) -> p t q r", t=4, r=8),
+            )
+
+        def consts_a():
+            nc.vector.tensor_scalar(out=half_sign[:], in0=p_cols, scalar1=0.0, scalar2=2.0, op0=ALU.is_ge, op1=ALU.mult)
+            nc.vector.tensor_scalar(out=neg[:], in0=p_cols, scalar1=-1.0, scalar2=2.0**-126, op0=ALU.mult, op1=ALU.max)
+            nc.vector.tensor_scalar(out=sign[:], in0=half_sign[:], scalar1=-1.0, scalar2=None, op0=ALU.add)
+            nc.vector.tensor_tensor(out=mag[:], in0=neg[:], in1=p_cols, op=ALU.max)
+            nc.vector.tensor_scalar(out=parts[:, 0, :], in0=mag[:], scalar1=2.0**-63, scalar2=2.0**64, op0=ALU.max, op1=ALU.min)
+            nc.vector.tensor_scalar(out=parts[:, 1, :], in0=mag[:], scalar1=2.0**63, scalar2=1.0, op0=ALU.mult, op1=ALU.min)
+            nc.vector.tensor_scalar(out=parts[:, 2, :], in0=mag[:], scalar1=2.0**-64, scalar2=1.0, op0=ALU.mult, op1=ALU.max)
+            nc.scalar.activation(out=logs[:], in_=parts[:], func=ACT.Ln)
+            nc.scalar.activation(out=probe[:, 1:2], in_=probe[:, 0:1], func=ACT.Exp)
+
+        def consts_b():
+            nc.vector.tensor_reduce(out=log_mag[:], in_=logs[:].rearrange("p s c -> p c s"), axis=mybir.AxisListType.X, op=ALU.add)
+
+        def consts_c():
+            nc.vector.tensor_tensor(out=bias[:], in0=log_mag[:], in1=e_cols, op=ALU.subtract)
+
+        units = unit_order()
+        due = {}
+
+        def later(k, job, *args):
+            due.setdefault(k, []).append((job, args))
+
+        later(0, sort_consts)
+        for k, unit in enumerate(units):
+            if unit[0] == "T":
+                later(max(SORT_MIN.get("%s%d%d" % unit[1:], 0), k - SORT_LEAD), sort_words, *unit[1:])
+            if unit[0] == "L" and unit[2] == 0:
+                later(max(0, k - USORT_LEAD), sort_u, unit[1])
+                later(max(1, k - USORT_LEAD), sort_us, unit[1])
+
+        turned = {}
+        lab_bf = {}
+        acc = {}
+
+        def unit_t(k, src, s, pair):
+            words = srt[(src, s, pair)][:].bitcast(F32)
+            for g in range(2):
+                if pair == 0:
+                    turned[(src, s, g)] = work.tile([P, 2048], BF16, name="turned", tag="turned", bufs=5, align_bytes=64)
+                bank = new_bank()
+                for u in range(2):
+                    for a in range(2):
+                        nc.tensor.transpose(
+                            bank[:, 256 * u + P * a : 256 * u + P * (a + 1)],
+                            words[:, u, 256 * a + P * g : 256 * a + P * (g + 1)],
+                            ident[:],
+                        )
+                dst = turned[(src, s, g)][:].bitcast(F32)
+                if src == "y":
+                    nc.scalar.copy(
+                        out=dst[:, 512 * pair : 512 * (pair + 1)].rearrange("p (n u) -> p n u", u=2),
+                        in_=bank[:].rearrange("p (u n) -> p n u", u=2),
+                    )
+                else:
+                    nc.scalar.copy(
+                        out=dst.rearrange("p (t h q r u) -> p h t q r u", t=4, h=2, r=8, u=2)[:, pair],
+                        in_=bank[:].rearrange("p (u q t r) -> p t q r u", u=2, t=4, r=8),
+                    )
+                if pair == 1:
+                    operands[(src, s, g)] = mx_operand("%s%d%d" % (src, s, g))
+                    later(k + QUANT_LAG + g, quantise, turned[(src, s, g)], operands[(src, s, g)])
+
+        def warm(n):
+            if n:
+                bank = new_bank()
+                for j in range(n):
+                    nc.tensor.matmul_mx(out=bank[:, 0:256], lhsT=warm_codes[:, 0:P].bitcast(FP8X4), lhsT_scale=warm_scales[:, 0:P], rhs=warm_codes[:].bitcast(FP8X4), rhs_scale=warm_scales[:], start=True, stop=True)
+
+        def unit_c(k):
+            warm(WARM)
+            bank = new_bank()
+            for t in range(4):
+                nc.tensor.transpose(bank[:, P * t : P * (t + 1)], c_sorted[:, P * t : P * (t + 1)], ident[:])
+            nc.scalar.copy(out=consts[:], in_=bank[:].rearrange("p (t c) -> p c t", t=4)[:, 0:8, :])
+            consts_a()
+            later(k + 2, consts_b)
+            later(k + 3, consts_c)
+            warm(WARM2)
+
+        def unit_l(k, G, c):
+            if c == 0:
+                lab_bf[G] = work.tile([P, 2048], BF16, name="lab_bf", tag="lab_bf", bufs=3, align_bytes=64)
+            bank = new_bank()
+            for t in range(4):
+                for g in range(2):
+                    nc.tensor.matmul_mx(
+                        out=bank[:, P * t : P * (t + 1)],
+                        lhsT=u_codes[G][:, 1024 * g + 256 * t : 1024 * g + 256 * (t + 1)].bitcast(FP4X4),
+                        lhsT_scale=u_sc[G][:, 512 * g + P * t : 512 * g + P * (t + 1)],
+                        rhs=v_codes[:, 1024 * g + 256 * c : 1024 * g + 256 * (c + 1)].bitcast(FP4X4),
+                        rhs_scale=vs[:, 512 * g + P * c : 512 * g + P * (c + 1)],
+                        start=(g == 0),
+                        stop=(g == 1),
+                    )
+            later(k + 1 + LEVAC_LAG, empty_l, bank, G, c)
+            if c == 3:
+                operands[("lab", G)] = mx_operand("lab%d" % G)
+                later(k + 2 + LEVAC_LAG + LAB_LAG, quantise, lab_bf[G], operands[("lab", G)])
+
+        def empty_l(bank, G, c):
+            nc.vector.tensor_tensor(
+                out=lab_bf[G][:, 512 * c : 512 * (c + 1)].rearrange("p (n t) -> p n t", t=4),
+                in0=bank[:].rearrange("p (t n) -> p n t", t=4),
+                in1=sign[:, 4 * G : 4 * G + 4].unsqueeze(1).to_broadcast([P, P, 4]),
+                op=ALU.mult,
+            )
+
+        def unit_i(k, h, G, t):
+            if t == 0:
+                like_bf[(h, G)] = work.tile([P, 4, 512], BF16, name="like_bf", tag="like_bf", bufs=6, align_bytes=64)
+            bank = new_bank()
+            for g in range(2):
+                x_codes, x_scales = operands[("x", G, g)]
+                y_codes, y_scales = operands[("y", h, g)]
+                nc.tensor.matmul_mx(
+                    out=bank[:],
+                    lhsT=x_codes[:, P * t : P * (t + 1)].bitcast(FP8X4),
+                    lhsT_scale=x_scales[:, P * t : P * (t + 1)],
+                    rhs=y_codes[:].bitcast(FP8X4),
+                    rhs_scale=y_scales[:],
+                    start=(g == 0),
+                    stop=(g == 1),
+                )
+            nc.scalar.activation(out=like_bf[(h, G)][:, t, :], in_=bank[:], func=ACT.Exp, bias=bias[:, 4 * G + t : 4 * G + t + 1])
+            if t == 3:
+                operands[("like", h, G)] = mx_operand("like%d%d" % (h, G))
+                later(k + 1 + WEAVE_LAG[h], weave, (h, G))
+                later(k + 1 + WQ_LAG + WEAVE_LAG[h], quantise_like, (h, G))
+
+        def unit_s(k, i, first, last, lo=0, hi=2):
+            span = slice(256 * lo, 256 * hi)
+            if first == 0:
+                acc[i] = new_bank()
+            for G in range(first, last):
+                like_codes, like_scales = operands[("like", i // 4, G)]
+                lab_codes, lab_scales = operands[("lab", G)]
+                cols = slice(P * (i % 4), P * (i % 4 + 1))
+                nc.tensor.matmul_mx(
+                    out=acc[i][:, span],
+                    lhsT=like_codes[:, cols].bitcast(FP8X4),
+                    lhsT_scale=like_scales[:, cols],
+                    rhs=lab_codes[:, span].bitcast(FP8X4),
+                    rhs_scale=lab_scales[:, span],
+                    start=(G == 0),
+                    stop=(G == 3),
+                )
+            if last == 4:
+                res = work.tile([P, B], F32, name="res", tag="res", bufs=6, align_bytes=64)
+                if i not in RES_V or hi == 1:
+                    nc.scalar.copy(out=res[:, span], in_=acc[i][:, span])
+                else:
+                    nc.vector.tensor_copy(out=res[:, span], in_=acc[i][:, span])
+                nc.sync.dma_start(out=out[P * i : P * (i + 1), span], in_=res[:, span])
+
+        emit = {"T": unit_t, "C": unit_c, "L": unit_l, "I": unit_i, "S": unit_s}
+        for k, unit in enumerate(units):
+            for job, args in due.get(k, []):
+                job(*args)
+            emit[unit[0]](k, *unit[1:])

@@ -18,53 +18,25 @@ ACT = mybir.ActivationFunctionType
 
 P = 128
 BANKS = 8
-SORT_LEAD = 3
-USORT_LEAD = 3
-QUANT_LAG = 2
-WEAVE_LAG = (10, 1)
-LAB_LAG = 1
-WARM = 3
-WARM2 = 6
-LEVAC_LAG = 1
-WQ_LAG = 2
-SORT_MIN = {}
-HEAD = "L00 L01 L02 L03 Ty00 L10 Ty01 L11 Tx00 L12 Tx01 L13 Tx10"
-SLOT = "T T I I L I I L"
-TAIL = "S004 S104 S204 S304 S403 S503 S434 S534 S604 S70401 S70412"
-P2 = {}
-LOADS = "v u0 us vs y00 u1 y01 x00 x01 x10 u2 x11 u3 x20 x21 x30 x31 y10 y11"
-SORT_ON_S = ("y00", "y01")
-RES_V = (1, 3, 5, 7)
-
-
-def unit_order():
-    def parse(w):
-        if w[0] == "T":
-            return ("T", w[1], int(w[2]), int(w[3]))
-        return (w[0],) + tuple(int(c) for c in w[1:])
-
-    u = [("C",)] + [parse(w) for w in HEAD.split()]
-    turns = [("T", "y", 0, 0), ("T", "y", 0, 1)] + [("T", "x", G, a) for G in range(4) for a in range(2)] + [("T", "y", 1, 0), ("T", "y", 1, 1)]
-    turns = [t for t in turns if t not in u]
-    labs = [("L", G, c) for G in range(4) for c in range(4)]
-    labs = [t for t in labs if t not in u]
-    ips = [("I", 0, G, t) for G in range(4) for t in range(4)]
-    for G in range(4):
-        for w in SLOT.split():
-            q = {"I": ips, "T": turns, "L": labs}[w]
-            if q:
-                u.append(q[0])
-                q.remove(q[0])
-    for G in range(4):
-        for t in range(4):
-            u.append(("I", 1, G, t))
-            if labs:
-                u.append(labs[0])
-                labs.remove(labs[0])
-            if (G, t) in P2:
-                u.append(parse(P2[(G, t)]))
-    u.extend([parse(w) for w in TAIL.split()])
-    return u
+WARM = 1
+CONST_G = 0
+LOADS = "c u0 v usa vs y00 y01 u1 x00 x01 usb u2 x10 x11 x20 x21 u3"
+SORT_ON_S = ("x01", "x11")
+RES_V = (5, 7)
+SRT_BUFS = 4
+LAB_BUFS = 3
+LIKE_BUFS = 6
+PROG = """
+W3 sc uc0 C us0 W5 ca L00 L01 oy00 xp e00 L02 oy01 cb L03 us1 uc1 Ty00 Ty01 e01 e02 e03 dx30 dx31
+L10 ox00 L11 ox01 dy10 dy11 L12 e10 L13 e11 uc2 us2
+Tx00 Tx01 e12 ox10 e13 L20 ox11 L21 qy00 L22 qx00 cc qy01 qx01
+Tx10 Tx11 e20 e21 e22 I000 ox20 I001 ox21 I002 I003 L23 
+qx10 qx11 Tx20 e23 Tx21 uc3 us3 ox30 ox31 I010 I011 I012 I013 l0 L30 L31 l1
+qx20 qx21 Tx30 e30 e31 Tx31 oy10 oy11 I020 w00 I021 I022 I023 L32 L33
+qx30 qx31 Ty10 e32 e33 Ty11 k00 I030 I031 I032 I033
+qy10 qy11 w01 I100 I101 w02 I102 k01 k02 I103 w03 l2 I110 I111 I112 I113 w10 k03 l3 I120 I121 I122 I123 k10 w11 I130 I131 I132 I133 w12 k11 k12
+S004 S104 w13 S204 k13 S304 S403 S503 S434 S534 S604 S70401 S70412
+"""
 
 
 def tile_soft_demapper_label_sums_s12_kernel(
@@ -91,25 +63,33 @@ def tile_soft_demapper_label_sums_s12_kernel(
             return kept(name + "_codes", [P, 512], U32), kept(name + "_scales", [P, 512], U8)
 
         c_raw = kept("c_raw", [8, 512], BF16)
-        nc.scalar.dma_start(out=c_raw[4:8, :], in_=prior.rearrange("(g c) -> g c", g=4))
-        nc.scalar.dma_start(out=c_raw[0:4, :], in_=energy.rearrange("(g c) -> g c", g=4))
+        us_a = kept("us_a", [P, 2 * 1024], U8)
+        us_b = kept("us_b", [P, 2 * 1024], U8)
+        vs = kept("vs", [P, 2 * B], U8)
+        nc.vector.memset(us_a[:].bitcast(I32), 0)
+        nc.vector.memset(vs[:].bitcast(I32), 0)
         probe = kept("probe", [P, 2], F32)
         nc.vector.memset(probe[:, 0:1], 1.0)
         nc.scalar.activation(out=probe[:, 1:2], in_=probe[:, 0:1], func=ACT.Ln)
-        us_raw = kept("us_raw", [P, 2 * NPTS], U8)
-        vs = kept("vs", [P, 2 * B], U8)
-        nc.vector.memset(us_raw[:].bitcast(I32), 0)
-        nc.vector.memset(vs[:].bitcast(I32), 0)
         c_sorted = kept("c_sorted", [P, 512], F32)
 
         ident = kept("ident", [P, P], F32)
         make_identity(nc, ident[:])
+        nc.gpsimd.memset(c_sorted[:], 0.0)
+
+        if WARM:
+            warm_bf = kept("warm_bf", [P, 1024], BF16)
+            nc.vector.memset(warm_bf[:].bitcast(I32), 0)
+            nc.vector.memset(us_b[:].bitcast(I32), 0)
+            warm_codes = kept("warm_codes", [P, 256], U32)
+            warm_scales = kept("warm_scales", [P, 256], U8)
+            nc.vector.quantize_mx(out=warm_codes[:].bitcast(FP8X4), scales=warm_scales[:], in_=warm_bf[:])
 
         raw = {}
 
         def load_rows(src, s, pair):
             rows = (y if src == "y" else points)[512 * s + 256 * pair : 512 * s + 256 * (pair + 1), :]
-            tile = kept("raw_%s%d%d" % (src, s, pair), [P, 2, D], BF16)
+            tile = work.tile([P, 2, D], BF16, name="raw_%s%d%d" % (src, s, pair), tag="raw", bufs=8, align_bytes=64)
             nc.sync.dma_start(out=tile[:], in_=rows.rearrange("(a p) d -> p a d", p=P))
             raw[(src, s, pair)] = tile
 
@@ -129,8 +109,13 @@ def tile_soft_demapper_label_sums_s12_kernel(
         for w in LOADS.split():
             if w == "v":
                 nc.sync.dma_start(out=v_codes[:].bitcast(I32).rearrange("p (g w) -> p g w", g=2), in_=v_words.bitcast(I32).rearrange("g p w -> p g w"))
-            elif w == "us":
-                load_scales(us_raw, u_scales)
+            elif w == "c":
+                nc.sync.dma_start(out=c_raw[4:8, :], in_=prior.rearrange("(g c) -> g c", g=4))
+                nc.sync.dma_start(out=c_raw[0:4, :], in_=energy.rearrange("(g c) -> g c", g=4))
+            elif w == "usa":
+                load_scales(us_a, u_scales[:, :, 0:1024])
+            elif w == "usb":
+                load_scales(us_b, u_scales[:, :, 1024:2048])
             elif w == "vs":
                 load_scales(vs, v_scales)
             elif w[0] == "u":
@@ -138,18 +123,10 @@ def tile_soft_demapper_label_sums_s12_kernel(
             else:
                 load_rows(w[0], int(w[1]), int(w[2]))
 
-        nc.gpsimd.memset(c_sorted[:], 0.0)
-        if WARM:
-            warm_bf = kept("warm_bf", [P, 1024], BF16)
-            nc.vector.memset(warm_bf[:].bitcast(I32), 0)
-            warm_codes = kept("warm_codes", [P, 256], U32)
-            warm_scales = kept("warm_scales", [P, 256], U8)
-            nc.vector.quantize_mx(out=warm_codes[:].bitcast(FP8X4), scales=warm_scales[:], in_=warm_bf[:])
-
         srt = {}
 
         def sort_words(src, s, pair):
-            tile = work.tile([P, 2, 2 * D // 2], BF16, name="srt", tag="srt", bufs=4, align_bytes=64)
+            tile = work.tile([P, 2, 2 * D // 2], BF16, name="srt", tag="srt", bufs=SRT_BUFS, align_bytes=64)
             copy = nc.scalar.copy if "%s%d%d" % (src, s, pair) in SORT_ON_S else nc.vector.tensor_copy
             copy(
                 out=tile[:].rearrange("p u (b e) -> p u b e", e=16),
@@ -172,7 +149,7 @@ def tile_soft_demapper_label_sums_s12_kernel(
             sc = kept("u_sc%d" % G, [P, 2 * 512], U8)
             nc.vector.tensor_copy(
                 out=sc[:].bitcast(I32).rearrange("p (g t q w) -> p g t q w", g=2, t=4, w=2),
-                in_=us_raw[:].bitcast(I32).rearrange("p (g G q t w) -> p G g t q w", g=2, G=4, t=4, w=2)[:, G],
+                in_=(us_b if G > 1 else us_a)[:].bitcast(I32).rearrange("p (g G q t w) -> p G g t q w", g=2, q=16, t=4, w=2)[:, G % 2],
             )
             u_sc[G] = sc
 
@@ -187,7 +164,7 @@ def tile_soft_demapper_label_sums_s12_kernel(
             quantise(woven[key], operands[("like",) + key])
 
         def weave(key):
-            dst = work.tile([P, 2048], BF16, name="woven", tag="woven", bufs=2, align_bytes=64)
+            dst = work.tile([P, 2048], BF16, name="woven", tag="woven", bufs=3, align_bytes=64)
             woven[key] = dst
             src = like_bf[key]
             nc.vector.tensor_copy(
@@ -222,7 +199,6 @@ def tile_soft_demapper_label_sums_s12_kernel(
             nc.vector.tensor_scalar(out=parts[:, 1, :], in0=mag[:], scalar1=2.0**63, scalar2=1.0, op0=ALU.mult, op1=ALU.min)
             nc.vector.tensor_scalar(out=parts[:, 2, :], in0=mag[:], scalar1=2.0**-64, scalar2=1.0, op0=ALU.mult, op1=ALU.max)
             nc.scalar.activation(out=logs[:], in_=parts[:], func=ACT.Ln)
-            nc.scalar.activation(out=probe[:, 1:2], in_=probe[:, 0:1], func=ACT.Exp)
 
         def consts_b():
             nc.vector.tensor_reduce(out=log_mag[:], in_=logs[:].rearrange("p s c -> p c s"), axis=mybir.AxisListType.X, op=ALU.add)
@@ -230,29 +206,19 @@ def tile_soft_demapper_label_sums_s12_kernel(
         def consts_c():
             nc.vector.tensor_tensor(out=bias[:], in0=log_mag[:], in1=e_cols, op=ALU.subtract)
 
-        units = unit_order()
-        due = {}
-
-        def later(k, job, *args):
-            due.setdefault(k, []).append((job, args))
-
-        later(0, sort_consts)
-        for k, unit in enumerate(units):
-            if unit[0] == "T":
-                later(max(SORT_MIN.get("%s%d%d" % unit[1:], 0), k - SORT_LEAD), sort_words, *unit[1:])
-            if unit[0] == "L" and unit[2] == 0:
-                later(max(0, k - USORT_LEAD), sort_u, unit[1])
-                later(max(1, k - USORT_LEAD), sort_us, unit[1])
-
         turned = {}
         lab_bf = {}
+        lbank = {}
         acc = {}
 
         def unit_t(k, src, s, pair):
             words = srt[(src, s, pair)][:].bitcast(F32)
             for g in range(2):
-                if pair == 0:
-                    turned[(src, s, g)] = work.tile([P, 2048], BF16, name="turned", tag="turned", bufs=5, align_bytes=64)
+                if pair == 0 and g == 0:
+                    both = work.tile([P, 4096], BF16, name="turned", tag="turned", bufs=3, align_bytes=64)
+                    turned[(src, s)] = both
+                    turned[(src, s, 0)] = both[:, 0:2048]
+                    turned[(src, s, 1)] = both[:, 2048:4096]
                 bank = new_bank()
                 for u in range(2):
                     for a in range(2):
@@ -272,9 +238,11 @@ def tile_soft_demapper_label_sums_s12_kernel(
                         out=dst.rearrange("p (t h q r u) -> p h t q r u", t=4, h=2, r=8, u=2)[:, pair],
                         in_=bank[:].rearrange("p (u q t r) -> p t q r u", u=2, t=4, r=8),
                     )
-                if pair == 1:
-                    operands[(src, s, g)] = mx_operand("%s%d%d" % (src, s, g))
-                    later(k + QUANT_LAG + g, quantise, turned[(src, s, g)], operands[(src, s, g)])
+                if pair == 1 and g == 0:
+                    cc = kept("%s%d_codes" % (src, s), [P, 1024], U32)
+                    ss = kept("%s%d_scales" % (src, s), [P, 1024], U8)
+                    for j in range(2):
+                        operands[(src, s, j)] = (cc[:, 512 * j : 512 * (j + 1)], ss[:, 512 * j : 512 * (j + 1)])
 
         def warm(n):
             if n:
@@ -283,19 +251,14 @@ def tile_soft_demapper_label_sums_s12_kernel(
                     nc.tensor.matmul_mx(out=bank[:, 0:256], lhsT=warm_codes[:, 0:P].bitcast(FP8X4), lhsT_scale=warm_scales[:, 0:P], rhs=warm_codes[:].bitcast(FP8X4), rhs_scale=warm_scales[:], start=True, stop=True)
 
         def unit_c(k):
-            warm(WARM)
             bank = new_bank()
             for t in range(4):
                 nc.tensor.transpose(bank[:, P * t : P * (t + 1)], c_sorted[:, P * t : P * (t + 1)], ident[:])
             nc.scalar.copy(out=consts[:], in_=bank[:].rearrange("p (t c) -> p c t", t=4)[:, 0:8, :])
-            consts_a()
-            later(k + 2, consts_b)
-            later(k + 3, consts_c)
-            warm(WARM2)
 
         def unit_l(k, G, c):
             if c == 0:
-                lab_bf[G] = work.tile([P, 2048], BF16, name="lab_bf", tag="lab_bf", bufs=3, align_bytes=64)
+                lab_bf[G] = work.tile([P, 2048], BF16, name="lab_bf", tag="lab_bf", bufs=LAB_BUFS, align_bytes=64)
             bank = new_bank()
             for t in range(4):
                 for g in range(2):
@@ -308,12 +271,12 @@ def tile_soft_demapper_label_sums_s12_kernel(
                         start=(g == 0),
                         stop=(g == 1),
                     )
-            later(k + 1 + LEVAC_LAG, empty_l, bank, G, c)
+            lbank[(G, c)] = bank
             if c == 3:
                 operands[("lab", G)] = mx_operand("lab%d" % G)
-                later(k + 2 + LEVAC_LAG + LAB_LAG, quantise, lab_bf[G], operands[("lab", G)])
 
-        def empty_l(bank, G, c):
+        def empty_l(G, c):
+            bank = lbank[(G, c)]
             nc.vector.tensor_tensor(
                 out=lab_bf[G][:, 512 * c : 512 * (c + 1)].rearrange("p (n t) -> p n t", t=4),
                 in0=bank[:].rearrange("p (t n) -> p n t", t=4),
@@ -321,9 +284,43 @@ def tile_soft_demapper_label_sums_s12_kernel(
                 op=ALU.mult,
             )
 
+        lab_rows = {}
+
+        def unit_m(G, t):
+            if t == 0:
+                lab_rows[G] = work.tile([P, 4, 512], BF16, name="lab_rows", tag="like_bf", bufs=LIKE_BUFS, align_bytes=64)
+            bank = new_bank()
+            for g in range(2):
+                nc.tensor.matmul_mx(
+                    out=bank[:],
+                    lhsT=u_codes[G][:, 1024 * g + 256 * t : 1024 * g + 256 * (t + 1)].bitcast(FP4X4),
+                    lhsT_scale=u_sc[G][:, 512 * g + P * t : 512 * g + P * (t + 1)],
+                    rhs=v_codes[:, 1024 * g : 1024 * (g + 1)].bitcast(FP4X4),
+                    rhs_scale=vs[:, 512 * g : 512 * (g + 1)],
+                    start=(g == 0),
+                    stop=(g == 1),
+                )
+            lbank[(G, t)] = bank
+
+        def empty_m(G, t, on_v):
+            bank = lbank[(G, t)]
+            if on_v:
+                nc.vector.tensor_scalar(out=lab_rows[G][:, t, :], in0=bank[:], scalar1=sign[:, 4 * G + t : 4 * G + t + 1], scalar2=None, op0=ALU.mult)
+            else:
+                nc.scalar.activation(out=lab_rows[G][:, t, :], in_=bank[:], func=ACT.Copy, scale=sign[:, 4 * G + t : 4 * G + t + 1])
+
+        def weave_m(G):
+            dst = work.tile([P, 2048], BF16, name="lab_bf", tag="lab_bf", bufs=LAB_BUFS, align_bytes=64)
+            lab_bf[G] = dst
+            operands[("lab", G)] = mx_operand("lab%d" % G)
+            nc.vector.tensor_copy(
+                out=dst[:].rearrange("p (c i t) -> p c t i", i=4, t=4),
+                in_=lab_rows[G][:].rearrange("p t (c i) -> p c t i", i=4),
+            )
+
         def unit_i(k, h, G, t):
             if t == 0:
-                like_bf[(h, G)] = work.tile([P, 4, 512], BF16, name="like_bf", tag="like_bf", bufs=6, align_bytes=64)
+                like_bf[(h, G)] = work.tile([P, 4, 512], BF16, name="like_bf", tag="like_bf", bufs=LIKE_BUFS, align_bytes=64)
             bank = new_bank()
             for g in range(2):
                 x_codes, x_scales = operands[("x", G, g)]
@@ -340,8 +337,6 @@ def tile_soft_demapper_label_sums_s12_kernel(
             nc.scalar.activation(out=like_bf[(h, G)][:, t, :], in_=bank[:], func=ACT.Exp, bias=bias[:, 4 * G + t : 4 * G + t + 1])
             if t == 3:
                 operands[("like", h, G)] = mx_operand("like%d%d" % (h, G))
-                later(k + 1 + WEAVE_LAG[h], weave, (h, G))
-                later(k + 1 + WQ_LAG + WEAVE_LAG[h], quantise_like, (h, G))
 
         def unit_s(k, i, first, last, lo=0, hi=2):
             span = slice(256 * lo, 256 * hi)
@@ -368,8 +363,53 @@ def tile_soft_demapper_label_sums_s12_kernel(
                     nc.vector.tensor_copy(out=res[:, span], in_=acc[i][:, span])
                 nc.sync.dma_start(out=out[P * i : P * (i + 1), span], in_=res[:, span])
 
-        emit = {"T": unit_t, "C": unit_c, "L": unit_l, "I": unit_i, "S": unit_s}
-        for k, unit in enumerate(units):
-            for job, args in due.get(k, []):
-                job(*args)
-            emit[unit[0]](k, *unit[1:])
+        for w in PROG.split():
+            n = [int(c) for c in w if c in "0123456789"]
+            if w[0] == "W":
+                warm(n[0])
+            elif w == "C":
+                unit_c(0)
+            elif w[0] == "T":
+                unit_t(0, w[1], *n)
+            elif w[0] == "L":
+                unit_l(0, *n)
+            elif w[0] == "M":
+                unit_m(*n)
+            elif w[0] == "E":
+                empty_m(n[0], n[1], False)
+            elif w[0] == "F":
+                empty_m(n[0], n[1], True)
+            elif w[0] == "z":
+                weave_m(*n)
+            elif w == "xp":
+                nc.scalar.activation(out=probe[:, 1:2], in_=logs[:, 1, 0:1], func=ACT.Exp)
+            elif w[0] == "I":
+                unit_i(0, *n)
+            elif w[0] == "S":
+                unit_s(0, *n)
+            elif w[0] == "d":
+                load_rows(w[1], *n)
+            elif w == "sc":
+                sort_consts()
+            elif w == "ca":
+                consts_a()
+            elif w == "cb":
+                consts_b()
+            elif w == "cc":
+                consts_c()
+            elif w[0:2] == "us":
+                sort_us(*n)
+            elif w[0:2] == "uc":
+                sort_u(*n)
+            elif w[0] == "o":
+                sort_words(w[1], *n)
+            elif w[0] == "e":
+                empty_l(*n)
+            elif w[0] == "q":
+                quantise(turned[(w[1], n[0], n[1])], operands[(w[1], n[0], n[1])])
+            elif w[0] == "l":
+                quantise(lab_bf[n[0]], operands[("lab", n[0])])
+            elif w[0] == "w":
+                weave(tuple(n))
+            elif w[0] == "k":
+                quantise_like(tuple(n))

@@ -17,26 +17,16 @@ ALU = mybir.AluOpType
 ACT = mybir.ActivationFunctionType
 
 P = 128
+SPAN = 512
+SLOTS = 4
 BANKS = 8
-WARM = 1
-CONST_G = 0
-LOADS = "c u0 v usa vs y00 y01 u1 x00 x01 usb u2 x10 x11 x20 x21 u3"
-SORT_ON_S = ("x01", "x11")
-RES_V = (5, 7)
-SRT_BUFS = 4
-LAB_BUFS = 3
-LIKE_BUFS = 6
-PROG = """
-W3 sc uc0 C us0 W5 ca L00 L01 oy00 xp e00 L02 oy01 cb L03 us1 uc1 Ty00 Ty01 e01 e02 e03 dx30 dx31
-L10 ox00 L11 ox01 dy10 dy11 L12 e10 L13 e11 uc2 us2
-Tx00 Tx01 e12 ox10 e13 L20 ox11 L21 qy00 L22 qx00 cc qy01 qx01
-Tx10 Tx11 e20 e21 e22 I000 ox20 I001 ox21 I002 I003 L23 
-qx10 qx11 Tx20 e23 Tx21 uc3 us3 ox30 ox31 I010 I011 I012 I013 l0 L30 L31 l1
-qx20 qx21 Tx30 e30 e31 Tx31 oy10 oy11 I020 w00 I021 I022 I023 L32 L33
-qx30 qx31 Ty10 e32 e33 Ty11 k00 I030 I031 I032 I033
-qy10 qy11 w01 I100 I101 w02 I102 k01 k02 I103 w03 l2 I110 I111 I112 I113 w10 k03 l3 I120 I121 I122 I123 k10 w11 I130 I131 I132 I133 w12 k11 k12
-S004 S104 w13 S204 k13 S304 S403 S503 S434 S534 S604 S70401 S70412
-"""
+RAW_BUFS = 8
+SORTED_BUFS = 4
+TURNED_BUFS = 3
+ROWS_BUFS = 6
+WOVEN_BUFS = 3
+RESULT_BUFS = 6
+WARM_BEFORE, WARM_AFTER = 3, 5
 
 
 def tile_soft_demapper_label_sums_s12_kernel(
@@ -45,371 +35,415 @@ def tile_soft_demapper_label_sums_s12_kernel(
     nc = tc.nc
     with ExitStack() as ctx:
         keep = ctx.enter_context(tc.tile_pool(name="keep", bufs=1))
-        work = ctx.enter_context(tc.tile_pool(name="work", bufs=3))
+        work = ctx.enter_context(tc.tile_pool(name="work", bufs=WOVEN_BUFS))
         psum = ctx.enter_context(tc.psum_pool(name="psum", bufs=1))
         ctx.enter_context(tc.manual_schedule())
 
         def kept(name, shape, dtype):
             return keep.tile(shape, dtype, name=name, align_bytes=64)
 
+        def streamed(name, shape, dtype, bufs):
+            return work.tile(shape, dtype, name=name, tag=name, bufs=bufs, align_bytes=64)
+
         banks = []
 
         def new_bank():
-            bank = psum.tile([P, 512], F32, name="bank%d" % len(banks), tag="bank%d" % (len(banks) % BANKS))
+            bank = psum.tile([P, SPAN], F32, name="bank%d" % len(banks), tag="bank%d" % (len(banks) % BANKS))
             banks.append(bank)
             return bank
 
-        def mx_operand(name):
-            return kept(name + "_codes", [P, 512], U32), kept(name + "_scales", [P, 512], U8)
+        def mx_tiles(name, width):
+            return kept(name + "_codes", [P, width], U32), kept(name + "_scales", [P, width], U8)
 
-        c_raw = kept("c_raw", [8, 512], BF16)
-        us_a = kept("us_a", [P, 2 * 1024], U8)
-        us_b = kept("us_b", [P, 2 * 1024], U8)
-        vs = kept("vs", [P, 2 * B], U8)
-        nc.vector.memset(us_a[:].bitcast(I32), 0)
-        nc.vector.memset(vs[:].bitcast(I32), 0)
+        def quantise(operand, values):
+            nc.vector.quantize_mx(out=operand[0].bitcast(FP8X4), scales=operand[1], in_=values)
+
+        def mx_pass(dst, lhs, rhs, dtype, first, last):
+            nc.tensor.matmul_mx(
+                out=dst,
+                lhsT=lhs[0].bitcast(dtype),
+                lhsT_scale=lhs[1],
+                rhs=rhs[0].bitcast(dtype),
+                rhs_scale=rhs[1],
+                start=first,
+                stop=last,
+            )
+
+        def columns(operand, lo, hi):
+            return operand[0][:, lo:hi], operand[1][:, lo:hi]
+
+        u_scale_rows = [kept("u_scale_rows%d" % k, [P, 2 * 2 * SPAN], U8) for k in range(2)]
+        v_scale_rows = kept("v_scale_rows", [P, 2 * B], U8)
+        nc.vector.memset(u_scale_rows[0][:].bitcast(I32), 0)
+        nc.vector.memset(v_scale_rows[:].bitcast(I32), 0)
         probe = kept("probe", [P, 2], F32)
         nc.vector.memset(probe[:, 0:1], 1.0)
         nc.scalar.activation(out=probe[:, 1:2], in_=probe[:, 0:1], func=ACT.Ln)
-        c_sorted = kept("c_sorted", [P, 512], F32)
-
         ident = kept("ident", [P, P], F32)
         make_identity(nc, ident[:])
-        nc.gpsimd.memset(c_sorted[:], 0.0)
-
-        if WARM:
-            warm_bf = kept("warm_bf", [P, 1024], BF16)
-            nc.vector.memset(warm_bf[:].bitcast(I32), 0)
-            nc.vector.memset(us_b[:].bitcast(I32), 0)
-            warm_codes = kept("warm_codes", [P, 256], U32)
-            warm_scales = kept("warm_scales", [P, 256], U8)
-            nc.vector.quantize_mx(out=warm_codes[:].bitcast(FP8X4), scales=warm_scales[:], in_=warm_bf[:])
+        const_rows = kept("const_rows", [P, SPAN], F32)
+        nc.gpsimd.memset(const_rows[:], 0.0)
+        warm_values = kept("warm_values", [P, SLOTS * 2 * P], BF16)
+        nc.vector.memset(warm_values[:].bitcast(I32), 0)
+        nc.vector.memset(u_scale_rows[1][:].bitcast(I32), 0)
+        warm = mx_tiles("warm", 2 * P)
+        quantise(columns(warm, 0, 2 * P), warm_values[:])
 
         raw = {}
-
-        def load_rows(src, s, pair):
-            rows = (y if src == "y" else points)[512 * s + 256 * pair : 512 * s + 256 * (pair + 1), :]
-            tile = work.tile([P, 2, D], BF16, name="raw_%s%d%d" % (src, s, pair), tag="raw", bufs=8, align_bytes=64)
-            nc.sync.dma_start(out=tile[:], in_=rows.rearrange("(a p) d -> p a d", p=P))
-            raw[(src, s, pair)] = tile
-
         u_raw = {}
 
+        def load_rows(tile, half):
+            src = y if tile[0] == "y" else points
+            row0 = SPAN * tile[1] + 2 * P * half
+            raw[tile, half] = streamed("raw", [P, 2, D], BF16, RAW_BUFS)
+            nc.sync.dma_start(out=raw[tile, half][:], in_=src[row0 : row0 + 2 * P, :].rearrange("(a p) d -> p a d", p=P))
+
         def load_u(G):
-            tile = kept("u_raw%d" % G, [P, 2, 256], I32)
-            nc.sync.dma_start(out=tile[:], in_=u_words.bitcast(I32).rearrange("g p w -> p g w")[:, :, 256 * G : 256 * (G + 1)])
-            u_raw[G] = tile
+            u_raw[G] = kept("u_raw%d" % G, [P, 2, 256], I32)
+            words = u_words.bitcast(I32).rearrange("g p w -> p g w")
+            nc.sync.dma_start(out=u_raw[G][:], in_=words[:, :, 256 * G : 256 * (G + 1)])
 
         def load_scales(plane, src):
             rows = src.bitcast(I32).rearrange("g (quad r) w -> r quad g w", r=4)
             for r in range(4):
                 nc.sync.dma_start(out=plane[r:P:32, :].bitcast(I32).rearrange("p (g w) -> p g w", g=2), in_=rows[r])
 
+        const_raw = kept("const_raw", [8, SPAN], BF16)
+        nc.sync.dma_start(out=const_raw[4:8, :], in_=prior.rearrange("(g c) -> g c", g=4))
+        nc.sync.dma_start(out=const_raw[0:4, :], in_=energy.rearrange("(g c) -> g c", g=4))
+        load_u(0)
         v_codes = kept("v_codes", [P, 2 * 2 * B], U8)
-        for w in LOADS.split():
-            if w == "v":
-                nc.sync.dma_start(out=v_codes[:].bitcast(I32).rearrange("p (g w) -> p g w", g=2), in_=v_words.bitcast(I32).rearrange("g p w -> p g w"))
-            elif w == "c":
-                nc.sync.dma_start(out=c_raw[4:8, :], in_=prior.rearrange("(g c) -> g c", g=4))
-                nc.sync.dma_start(out=c_raw[0:4, :], in_=energy.rearrange("(g c) -> g c", g=4))
-            elif w == "usa":
-                load_scales(us_a, u_scales[:, :, 0:1024])
-            elif w == "usb":
-                load_scales(us_b, u_scales[:, :, 1024:2048])
-            elif w == "vs":
-                load_scales(vs, v_scales)
-            elif w[0] == "u":
-                load_u(int(w[1]))
-            else:
-                load_rows(w[0], int(w[1]), int(w[2]))
+        nc.sync.dma_start(
+            out=v_codes[:].bitcast(I32).rearrange("p (g w) -> p g w", g=2),
+            in_=v_words.bitcast(I32).rearrange("g p w -> p g w"),
+        )
+        load_scales(u_scale_rows[0], u_scales[:, :, 0 : 2 * SPAN])
+        load_scales(v_scale_rows, v_scales)
+        load_rows(("y", 0), 0)
+        load_rows(("y", 0), 1)
+        load_u(1)
+        load_rows(("x", 0), 0)
+        load_rows(("x", 0), 1)
+        load_rows(("x", 1), 0)
+        load_scales(u_scale_rows[1], u_scales[:, :, 2 * SPAN : 4 * SPAN])
+        load_u(2)
+        load_rows(("x", 1), 1)
+        load_rows(("x", 2), 0)
+        load_rows(("x", 2), 1)
+        load_u(3)
 
-        srt = {}
+        sorted_rows = {}
+        turned = {}
+        rows_mx = {}
 
-        def sort_words(src, s, pair):
-            tile = work.tile([P, 2, 2 * D // 2], BF16, name="srt", tag="srt", bufs=SRT_BUFS, align_bytes=64)
-            copy = nc.scalar.copy if "%s%d%d" % (src, s, pair) in SORT_ON_S else nc.vector.tensor_copy
+        def sort_rows(tile, half, copy=nc.vector.tensor_copy):
+            dst = streamed("sorted_rows", [P, 2, D], BF16, SORTED_BUFS)
             copy(
-                out=tile[:].rearrange("p u (b e) -> p u b e", e=16),
-                in_=raw[(src, s, pair)][:].rearrange("p a (b u e) -> p u (a b) e", u=2, e=16),
+                out=dst[:].rearrange("p u (b e) -> p u b e", e=16),
+                in_=raw[tile, half][:].rearrange("p a (b u e) -> p u (a b) e", u=2, e=16),
             )
-            srt[(src, s, pair)] = tile
+            sorted_rows[tile, half] = dst
 
-        u_codes = {}
-        u_sc = {}
+        def turn(tile):
+            turned[tile] = streamed("turned", [P, 2 * SLOTS * SPAN], BF16, TURNED_BUFS)
+            rows_mx[tile] = mx_tiles("%s%d" % tile, 2 * SPAN)
+            for half in range(2):
+                words = sorted_rows[tile, half][:].bitcast(F32)
+                for g in range(2):
+                    bank = new_bank()
+                    for u in range(2):
+                        for a in range(2):
+                            nc.tensor.transpose(
+                                bank[:, 2 * P * u + P * a : 2 * P * u + P * (a + 1)],
+                                words[:, u, 2 * P * a + P * g : 2 * P * a + P * (g + 1)],
+                                ident[:],
+                            )
+                    dst = turned[tile][:, SLOTS * SPAN * g : SLOTS * SPAN * (g + 1)].bitcast(F32)
+                    if tile[0] == "y":
+                        nc.scalar.copy(
+                            out=dst[:, SPAN * half : SPAN * (half + 1)].rearrange("p (n u) -> p n u", u=2),
+                            in_=bank[:].rearrange("p (u n) -> p n u", u=2),
+                        )
+                    else:
+                        nc.scalar.copy(
+                            out=dst.rearrange("p (t h q r u) -> p h t q r u", t=4, h=2, r=8, u=2)[:, half],
+                            in_=bank[:].rearrange("p (u q t r) -> p t q r u", u=2, t=4, r=8),
+                        )
 
-        def sort_u(G):
-            codes = kept("u_codes%d" % G, [P, 2 * 1024], U8)
-            nc.vector.tensor_copy(
-                out=codes[:].bitcast(I32).rearrange("p (g t q w) -> p g t q w", g=2, t=4, w=4),
-                in_=u_raw[G][:].rearrange("p g (q t w) -> p g t q w", t=4, w=4),
-            )
-            u_codes[G] = codes
+        def quantise_rows(tile):
+            quantise(columns(rows_mx[tile], 0, 2 * SPAN), turned[tile][:])
 
-        def sort_us(G):
-            sc = kept("u_sc%d" % G, [P, 2 * 512], U8)
-            nc.vector.tensor_copy(
-                out=sc[:].bitcast(I32).rearrange("p (g t q w) -> p g t q w", g=2, t=4, w=2),
-                in_=(us_b if G > 1 else us_a)[:].bitcast(I32).rearrange("p (g G q t w) -> p G g t q w", g=2, q=16, t=4, w=2)[:, G % 2],
-            )
-            u_sc[G] = sc
-
-        def quantise(tile, operand):
-            nc.vector.quantize_mx(out=operand[0][:].bitcast(FP8X4), scales=operand[1][:], in_=tile[:])
-
-        woven = {}
-        like_bf = {}
-        operands = {}
-
-        def quantise_like(key):
-            quantise(woven[key], operands[("like",) + key])
-
-        def weave(key):
-            dst = work.tile([P, 2048], BF16, name="woven", tag="woven", bufs=3, align_bytes=64)
-            woven[key] = dst
-            src = like_bf[key]
-            nc.vector.tensor_copy(
-                out=dst[:].rearrange("p (c i t) -> p c t i", i=4, t=4),
-                in_=src[:].rearrange("p t (c i) -> p c t i", i=4),
-            )
-
-        consts = kept("consts", [P, 8, 4], F32)
+        consts = kept("consts", [P, 8, SLOTS], F32)
+        energy_cols = consts[:, 0:4, :].rearrange("p g t -> p (g t)")
+        prior_cols = consts[:, 4:8, :].rearrange("p g t -> p (g t)")
+        magnitude = kept("magnitude", [P, 16], F32)
+        twice_positive = kept("twice_positive", [P, 16], F32)
         sign = kept("sign", [P, 16], F32)
-        half_sign = kept("half_sign", [P, 16], F32)
-        neg = kept("neg", [P, 16], F32)
-        mag = kept("mag", [P, 16], F32)
-        parts = kept("parts", [P, 3, 16], F32)
+        factors = kept("factors", [P, 3, 16], F32)
         logs = kept("logs", [P, 3, 16], F32)
-        log_mag = kept("log_mag", [P, 16], F32)
+        log_prior = kept("log_prior", [P, 16], F32)
         bias = kept("bias", [P, 16], F32)
-        e_cols = consts[:, 0:4, :].rearrange("p g t -> p (g t)")
-        p_cols = consts[:, 4:8, :].rearrange("p g t -> p (g t)")
 
         def sort_consts():
             nc.vector.tensor_copy(
-                out=c_sorted[0:8, :].rearrange("p (t q r) -> p t q r", t=4, r=8),
-                in_=c_raw[:].rearrange("p (q t r) -> p t q r", t=4, r=8),
+                out=const_rows[0:8, :].rearrange("p (t q r) -> p t q r", t=4, r=8),
+                in_=const_raw[:].rearrange("p (q t r) -> p t q r", t=4, r=8),
             )
 
-        def consts_a():
-            nc.vector.tensor_scalar(out=half_sign[:], in0=p_cols, scalar1=0.0, scalar2=2.0, op0=ALU.is_ge, op1=ALU.mult)
-            nc.vector.tensor_scalar(out=neg[:], in0=p_cols, scalar1=-1.0, scalar2=2.0**-126, op0=ALU.mult, op1=ALU.max)
-            nc.vector.tensor_scalar(out=sign[:], in0=half_sign[:], scalar1=-1.0, scalar2=None, op0=ALU.add)
-            nc.vector.tensor_tensor(out=mag[:], in0=neg[:], in1=p_cols, op=ALU.max)
-            nc.vector.tensor_scalar(out=parts[:, 0, :], in0=mag[:], scalar1=2.0**-63, scalar2=2.0**64, op0=ALU.max, op1=ALU.min)
-            nc.vector.tensor_scalar(out=parts[:, 1, :], in0=mag[:], scalar1=2.0**63, scalar2=1.0, op0=ALU.mult, op1=ALU.min)
-            nc.vector.tensor_scalar(out=parts[:, 2, :], in0=mag[:], scalar1=2.0**-64, scalar2=1.0, op0=ALU.mult, op1=ALU.max)
-            nc.scalar.activation(out=logs[:], in_=parts[:], func=ACT.Ln)
-
-        def consts_b():
-            nc.vector.tensor_reduce(out=log_mag[:], in_=logs[:].rearrange("p s c -> p c s"), axis=mybir.AxisListType.X, op=ALU.add)
-
-        def consts_c():
-            nc.vector.tensor_tensor(out=bias[:], in0=log_mag[:], in1=e_cols, op=ALU.subtract)
-
-        turned = {}
-        lab_bf = {}
-        lbank = {}
-        acc = {}
-
-        def unit_t(k, src, s, pair):
-            words = srt[(src, s, pair)][:].bitcast(F32)
-            for g in range(2):
-                if pair == 0 and g == 0:
-                    both = work.tile([P, 4096], BF16, name="turned", tag="turned", bufs=3, align_bytes=64)
-                    turned[(src, s)] = both
-                    turned[(src, s, 0)] = both[:, 0:2048]
-                    turned[(src, s, 1)] = both[:, 2048:4096]
-                bank = new_bank()
-                for u in range(2):
-                    for a in range(2):
-                        nc.tensor.transpose(
-                            bank[:, 256 * u + P * a : 256 * u + P * (a + 1)],
-                            words[:, u, 256 * a + P * g : 256 * a + P * (g + 1)],
-                            ident[:],
-                        )
-                dst = turned[(src, s, g)][:].bitcast(F32)
-                if src == "y":
-                    nc.scalar.copy(
-                        out=dst[:, 512 * pair : 512 * (pair + 1)].rearrange("p (n u) -> p n u", u=2),
-                        in_=bank[:].rearrange("p (u n) -> p n u", u=2),
-                    )
-                else:
-                    nc.scalar.copy(
-                        out=dst.rearrange("p (t h q r u) -> p h t q r u", t=4, h=2, r=8, u=2)[:, pair],
-                        in_=bank[:].rearrange("p (u q t r) -> p t q r u", u=2, t=4, r=8),
-                    )
-                if pair == 1 and g == 0:
-                    cc = kept("%s%d_codes" % (src, s), [P, 1024], U32)
-                    ss = kept("%s%d_scales" % (src, s), [P, 1024], U8)
-                    for j in range(2):
-                        operands[(src, s, j)] = (cc[:, 512 * j : 512 * (j + 1)], ss[:, 512 * j : 512 * (j + 1)])
-
-        def warm(n):
-            if n:
-                bank = new_bank()
-                for j in range(n):
-                    nc.tensor.matmul_mx(out=bank[:, 0:256], lhsT=warm_codes[:, 0:P].bitcast(FP8X4), lhsT_scale=warm_scales[:, 0:P], rhs=warm_codes[:].bitcast(FP8X4), rhs_scale=warm_scales[:], start=True, stop=True)
-
-        def unit_c(k):
+        def turn_consts():
             bank = new_bank()
-            for t in range(4):
-                nc.tensor.transpose(bank[:, P * t : P * (t + 1)], c_sorted[:, P * t : P * (t + 1)], ident[:])
+            for t in range(SLOTS):
+                nc.tensor.transpose(bank[:, P * t : P * (t + 1)], const_rows[:, P * t : P * (t + 1)], ident[:])
             nc.scalar.copy(out=consts[:], in_=bank[:].rearrange("p (t c) -> p c t", t=4)[:, 0:8, :])
 
-        def unit_l(k, G, c):
-            if c == 0:
-                lab_bf[G] = work.tile([P, 2048], BF16, name="lab_bf", tag="lab_bf", bufs=LAB_BUFS, align_bytes=64)
-            bank = new_bank()
-            for t in range(4):
-                for g in range(2):
-                    nc.tensor.matmul_mx(
-                        out=bank[:, P * t : P * (t + 1)],
-                        lhsT=u_codes[G][:, 1024 * g + 256 * t : 1024 * g + 256 * (t + 1)].bitcast(FP4X4),
-                        lhsT_scale=u_sc[G][:, 512 * g + P * t : 512 * g + P * (t + 1)],
-                        rhs=v_codes[:, 1024 * g + 256 * c : 1024 * g + 256 * (c + 1)].bitcast(FP4X4),
-                        rhs_scale=vs[:, 512 * g + P * c : 512 * g + P * (c + 1)],
-                        start=(g == 0),
-                        stop=(g == 1),
-                    )
-            lbank[(G, c)] = bank
-            if c == 3:
-                operands[("lab", G)] = mx_operand("lab%d" % G)
+        def sign_and_logs():
+            nc.vector.scalar_tensor_tensor(
+                out=magnitude[:], in0=prior_cols, scalar=-1.0, in1=prior_cols, op0=ALU.mult, op1=ALU.max
+            )
+            nc.vector.tensor_scalar(
+                out=twice_positive[:], in0=prior_cols, scalar1=0.0, scalar2=2.0, op0=ALU.is_ge, op1=ALU.mult
+            )
+            for k, (s1, s2, op0, op1) in enumerate(
+                (
+                    (2.0**-63, 2.0**64, ALU.max, ALU.min),
+                    (2.0**-126, 2.0**-63, ALU.max, ALU.min),
+                    (2.0**-64, 1.0, ALU.mult, ALU.max),
+                )
+            ):
+                nc.vector.tensor_scalar(out=factors[:, k, :], in0=magnitude[:], scalar1=s1, scalar2=s2, op0=op0, op1=op1)
+            nc.vector.tensor_scalar(out=sign[:], in0=twice_positive[:], scalar1=-1.0, scalar2=None, op0=ALU.add)
+            nc.scalar.activation(out=logs[:, 1, :], in_=factors[:, 1, :], func=ACT.Ln, scale=2.0**63)
+            nc.scalar.activation(out=logs[:, 0:3:2, :], in_=factors[:, 0:3:2, :], func=ACT.Ln)
 
-        def empty_l(G, c):
-            bank = lbank[(G, c)]
+        def sum_logs():
+            nc.vector.tensor_reduce(
+                out=log_prior[:], in_=logs[:].rearrange("p s c -> p c s"), axis=mybir.AxisListType.X, op=ALU.add
+            )
+
+        def make_bias():
+            nc.vector.tensor_tensor(out=bias[:], in0=log_prior[:], in1=energy_cols, op=ALU.subtract)
+
+        def weave(dst, rows, lo, hi, copy=nc.vector.tensor_copy):
+            copy(
+                out=dst[:, SLOTS * lo : SLOTS * hi].rearrange("p (c i t) -> p c t i", i=4, t=4),
+                in_=rows[:, :, lo:hi].rearrange("p t (c i) -> p c t i", i=4),
+            )
+
+        u_codes = {}
+        u_planes = {}
+        label_banks = {}
+        label_rows = {}
+        label_woven = {}
+        label_mx = {}
+
+        def sort_u_codes(G):
+            u_codes[G] = kept("u_codes%d" % G, [P, 2 * 2 * SPAN], U8)
+            nc.vector.tensor_copy(
+                out=u_codes[G][:].bitcast(I32).rearrange("p (g t q w) -> p g t q w", g=2, t=4, w=4),
+                in_=u_raw[G][:].rearrange("p g (q t w) -> p g t q w", t=4, w=4),
+            )
+
+        def sort_u_scales(G):
+            u_planes[G] = kept("u_plane%d" % G, [P, 2 * SPAN], U8)
+            both = u_scale_rows[G // 2][:].bitcast(I32).rearrange("p (g k q t w) -> p k g t q w", g=2, q=16, t=4, w=2)
+            nc.vector.tensor_copy(
+                out=u_planes[G][:].bitcast(I32).rearrange("p (g t q w) -> p g t q w", g=2, t=4, w=2),
+                in_=both[:, G % 2],
+            )
+
+        def u_operand(G, g, t):
+            lo = SPAN * g + P * t
+            return u_codes[G][:, 2 * lo : 2 * (lo + P)], u_planes[G][:, lo : lo + P]
+
+        def v_operand(g, lo, hi):
+            return v_codes[:, 2 * (B * g + lo) : 2 * (B * g + hi)], v_scale_rows[:, B * g + lo : B * g + hi]
+
+        def labels_wide(G, t):
+            if t == 0:
+                label_rows[G] = streamed("rows", [P, SLOTS, SPAN], BF16, ROWS_BUFS)
+            bank = new_bank()
+            for g in range(2):
+                mx_pass(bank[:], u_operand(G, g, t), v_operand(g, 0, B), FP4X4, g == 0, g == 1)
+            col = SLOTS * G + t
+            nc.scalar.activation(out=label_rows[G][:, t, :], in_=bank[:], func=ACT.Copy, scale=sign[:, col : col + 1])
+
+        def weave_labels(G):
+            label_woven[G] = streamed("label_woven", [P, SLOTS * B], BF16, WOVEN_BUFS)
+            weave(label_woven[G], label_rows[G], 0, B)
+
+        def labels_narrow(G, c):
+            if c == 0:
+                label_woven[G] = streamed("label_woven", [P, SLOTS * B], BF16, WOVEN_BUFS)
+            bank = new_bank()
+            for t in range(SLOTS):
+                for g in range(2):
+                    mx_pass(
+                        bank[:, P * t : P * (t + 1)], u_operand(G, g, t), v_operand(g, P * c, P * (c + 1)), FP4X4, g == 0, g == 1
+                    )
+            label_banks[G, c] = bank
+
+        def empty_labels(G, c):
             nc.vector.tensor_tensor(
-                out=lab_bf[G][:, 512 * c : 512 * (c + 1)].rearrange("p (n t) -> p n t", t=4),
-                in0=bank[:].rearrange("p (t n) -> p n t", t=4),
-                in1=sign[:, 4 * G : 4 * G + 4].unsqueeze(1).to_broadcast([P, P, 4]),
+                out=label_woven[G][:, SPAN * c : SPAN * (c + 1)].rearrange("p (n t) -> p n t", t=4),
+                in0=label_banks[G, c][:].rearrange("p (t n) -> p n t", t=4),
+                in1=sign[:, SLOTS * G : SLOTS * (G + 1)].unsqueeze(1).to_broadcast([P, P, SLOTS]),
                 op=ALU.mult,
             )
 
-        lab_rows = {}
+        def quantise_labels(G):
+            label_mx[G] = mx_tiles("label%d" % G, B)
+            quantise(columns(label_mx[G], 0, B), label_woven[G][:])
 
-        def unit_m(G, t):
-            if t == 0:
-                lab_rows[G] = work.tile([P, 4, 512], BF16, name="lab_rows", tag="like_bf", bufs=LIKE_BUFS, align_bytes=64)
+        like_rows = {}
+        like_woven = {}
+        like_mx = {}
+
+        def like(h, G):
+            like_rows[h, G] = streamed("rows", [P, SLOTS, SPAN], BF16, ROWS_BUFS)
+            like_mx[h, G] = mx_tiles("like%d%d" % (h, G), SPAN)
+            for t in range(SLOTS):
+                bank = new_bank()
+                for g in range(2):
+                    lhs = columns(rows_mx["x", G], SPAN * g + P * t, SPAN * g + P * (t + 1))
+                    rhs = columns(rows_mx["y", h], SPAN * g, SPAN * (g + 1))
+                    mx_pass(bank[:], lhs, rhs, FP8X4, g == 0, g == 1)
+                col = SLOTS * G + t
+                nc.scalar.activation(out=like_rows[h, G][:, t, :], in_=bank[:], func=ACT.Exp, bias=bias[:, col : col + 1])
+
+        def weave_like(h, G, lo=0, hi=SPAN, copy=nc.vector.tensor_copy):
+            if lo == 0:
+                like_woven[h, G] = streamed("like_woven", [P, SLOTS * SPAN], BF16, WOVEN_BUFS)
+            weave(like_woven[h, G], like_rows[h, G], lo, hi, copy)
+
+        def quantise_like(h, G, lo=0, hi=SPAN):
+            quantise(columns(like_mx[h, G], lo, hi), like_woven[h, G][:, SLOTS * lo : SLOTS * hi])
+
+        sums = {}
+
+        def output_passes(i, groups, lo=0, hi=B, copy=nc.scalar.copy):
+            if groups[0] == 0:
+                sums[i] = new_bank()
+            for G in groups:
+                lhs = columns(like_mx[i // 4, G], P * (i % 4), P * (i % 4 + 1))
+                mx_pass(sums[i][:, lo:hi], lhs, columns(label_mx[G], lo, hi), FP8X4, G == 0, G == 3)
+            if groups[-1] == 3:
+                result = streamed("result", [P, B], F32, RESULT_BUFS)
+                copy(out=result[:, lo:hi], in_=sums[i][:, lo:hi])
+                nc.sync.dma_start(out=out[P * i : P * (i + 1), lo:hi], in_=result[:, lo:hi])
+
+        def warm_up(passes):
             bank = new_bank()
-            for g in range(2):
-                nc.tensor.matmul_mx(
-                    out=bank[:],
-                    lhsT=u_codes[G][:, 1024 * g + 256 * t : 1024 * g + 256 * (t + 1)].bitcast(FP4X4),
-                    lhsT_scale=u_sc[G][:, 512 * g + P * t : 512 * g + P * (t + 1)],
-                    rhs=v_codes[:, 1024 * g : 1024 * (g + 1)].bitcast(FP4X4),
-                    rhs_scale=vs[:, 512 * g : 512 * (g + 1)],
-                    start=(g == 0),
-                    stop=(g == 1),
-                )
-            lbank[(G, t)] = bank
+            for k in range(passes):
+                mx_pass(bank[:, 0 : 2 * P], columns(warm, 0, P), columns(warm, 0, 2 * P), FP8X4, True, True)
 
-        def empty_m(G, t, on_v):
-            bank = lbank[(G, t)]
-            if on_v:
-                nc.vector.tensor_scalar(out=lab_rows[G][:, t, :], in0=bank[:], scalar1=sign[:, 4 * G + t : 4 * G + t + 1], scalar2=None, op0=ALU.mult)
-            else:
-                nc.scalar.activation(out=lab_rows[G][:, t, :], in_=bank[:], func=ACT.Copy, scale=sign[:, 4 * G + t : 4 * G + t + 1])
 
-        def weave_m(G):
-            dst = work.tile([P, 2048], BF16, name="lab_bf", tag="lab_bf", bufs=LAB_BUFS, align_bytes=64)
-            lab_bf[G] = dst
-            operands[("lab", G)] = mx_operand("lab%d" % G)
-            nc.vector.tensor_copy(
-                out=dst[:].rearrange("p (c i t) -> p c t i", i=4, t=4),
-                in_=lab_rows[G][:].rearrange("p t (c i) -> p c t i", i=4),
-            )
+        warm_up(WARM_BEFORE)
+        sort_consts()
+        sort_u_codes(0)
+        turn_consts()
+        sort_u_scales(0)
+        warm_up(WARM_AFTER)
+        sign_and_logs()
+        for half in range(2):
+            labels_wide(0, 2 * half)
+            labels_wide(0, 2 * half + 1)
+            sort_rows(("y", 0), half)
+        sort_u_scales(1)
+        sort_u_codes(1)
 
-        def unit_i(k, h, G, t):
-            if t == 0:
-                like_bf[(h, G)] = work.tile([P, 4, 512], BF16, name="like_bf", tag="like_bf", bufs=LIKE_BUFS, align_bytes=64)
-            bank = new_bank()
-            for g in range(2):
-                x_codes, x_scales = operands[("x", G, g)]
-                y_codes, y_scales = operands[("y", h, g)]
-                nc.tensor.matmul_mx(
-                    out=bank[:],
-                    lhsT=x_codes[:, P * t : P * (t + 1)].bitcast(FP8X4),
-                    lhsT_scale=x_scales[:, P * t : P * (t + 1)],
-                    rhs=y_codes[:].bitcast(FP8X4),
-                    rhs_scale=y_scales[:],
-                    start=(g == 0),
-                    stop=(g == 1),
-                )
-            nc.scalar.activation(out=like_bf[(h, G)][:, t, :], in_=bank[:], func=ACT.Exp, bias=bias[:, 4 * G + t : 4 * G + t + 1])
-            if t == 3:
-                operands[("like", h, G)] = mx_operand("like%d%d" % (h, G))
+        turn(("y", 0))
+        nc.scalar.activation(out=probe[:, 1:2], in_=logs[:, 1, 0:1], func=ACT.Exp)
+        sum_logs()
+        load_rows(("y", 1), 0)
+        load_rows(("y", 1), 1)
+        labels_narrow(1, 0)
+        sort_rows(("x", 0), 0)
+        labels_narrow(1, 1)
+        empty_labels(1, 0)
+        sort_rows(("x", 0), 1)
+        load_rows(("x", 3), 0)
+        load_rows(("x", 3), 1)
+        labels_narrow(1, 2)
+        labels_narrow(1, 3)
+        quantise_rows(("y", 0))
+        sort_u_codes(2)
+        sort_u_scales(2)
 
-        def unit_s(k, i, first, last, lo=0, hi=2):
-            span = slice(256 * lo, 256 * hi)
-            if first == 0:
-                acc[i] = new_bank()
-            for G in range(first, last):
-                like_codes, like_scales = operands[("like", i // 4, G)]
-                lab_codes, lab_scales = operands[("lab", G)]
-                cols = slice(P * (i % 4), P * (i % 4 + 1))
-                nc.tensor.matmul_mx(
-                    out=acc[i][:, span],
-                    lhsT=like_codes[:, cols].bitcast(FP8X4),
-                    lhsT_scale=like_scales[:, cols],
-                    rhs=lab_codes[:, span].bitcast(FP8X4),
-                    rhs_scale=lab_scales[:, span],
-                    start=(G == 0),
-                    stop=(G == 3),
-                )
-            if last == 4:
-                res = work.tile([P, B], F32, name="res", tag="res", bufs=6, align_bytes=64)
-                if i not in RES_V or hi == 1:
-                    nc.scalar.copy(out=res[:, span], in_=acc[i][:, span])
-                else:
-                    nc.vector.tensor_copy(out=res[:, span], in_=acc[i][:, span])
-                nc.sync.dma_start(out=out[P * i : P * (i + 1), span], in_=res[:, span])
+        turn(("x", 0))
+        empty_labels(1, 1)
+        sort_rows(("x", 1), 0)
+        empty_labels(1, 2)
+        labels_narrow(2, 0)
+        labels_narrow(2, 1)
+        empty_labels(1, 3)
+        sort_rows(("x", 1), 1, nc.scalar.copy)
+        labels_narrow(2, 2)
+        make_bias()
+        quantise_rows(("x", 0))
 
-        for w in PROG.split():
-            n = [int(c) for c in w if c in "0123456789"]
-            if w[0] == "W":
-                warm(n[0])
-            elif w == "C":
-                unit_c(0)
-            elif w[0] == "T":
-                unit_t(0, w[1], *n)
-            elif w[0] == "L":
-                unit_l(0, *n)
-            elif w[0] == "M":
-                unit_m(*n)
-            elif w[0] == "E":
-                empty_m(n[0], n[1], False)
-            elif w[0] == "F":
-                empty_m(n[0], n[1], True)
-            elif w[0] == "z":
-                weave_m(*n)
-            elif w == "xp":
-                nc.scalar.activation(out=probe[:, 1:2], in_=logs[:, 1, 0:1], func=ACT.Exp)
-            elif w[0] == "I":
-                unit_i(0, *n)
-            elif w[0] == "S":
-                unit_s(0, *n)
-            elif w[0] == "d":
-                load_rows(w[1], *n)
-            elif w == "sc":
-                sort_consts()
-            elif w == "ca":
-                consts_a()
-            elif w == "cb":
-                consts_b()
-            elif w == "cc":
-                consts_c()
-            elif w[0:2] == "us":
-                sort_us(*n)
-            elif w[0:2] == "uc":
-                sort_u(*n)
-            elif w[0] == "o":
-                sort_words(w[1], *n)
-            elif w[0] == "e":
-                empty_l(*n)
-            elif w[0] == "q":
-                quantise(turned[(w[1], n[0], n[1])], operands[(w[1], n[0], n[1])])
-            elif w[0] == "l":
-                quantise(lab_bf[n[0]], operands[("lab", n[0])])
-            elif w[0] == "w":
-                weave(tuple(n))
-            elif w[0] == "k":
-                quantise_like(tuple(n))
+        def one_round(tile, following, group, full_banks, new_banks, before, after):
+            turn(tile)
+            for bank_key in full_banks:
+                empty_labels(*bank_key)
+            for half in range(2 if following else 0):
+                sort_rows(following, half)
+            like(*group)
+            before()
+            for bank_key in new_banks:
+                labels_narrow(*bank_key)
+            quantise_rows(tile)
+            after()
+
+        one_round(
+            ("x", 1), ("x", 2), (0, 0), [(2, 0), (2, 1), (2, 2)], [(2, 3)],
+            lambda: sort_u_codes(3), lambda: sort_u_scales(3),
+        )
+        one_round(
+            ("x", 2), ("y", 1), (0, 1), [(2, 3)], [(3, 0), (3, 1)],
+            lambda: weave_like(0, 0), lambda: quantise_labels(1),
+        )
+        one_round(
+            ("y", 1), ("x", 3), (0, 2), [(3, 0), (3, 1)], [(3, 2), (3, 3)],
+            lambda: weave_labels(0), lambda: quantise_like(0, 0),
+        )
+        one_round(
+            ("x", 3), None, (1, 0), [(3, 2), (3, 3)], [],
+            lambda: weave_like(0, 1), lambda: quantise_labels(0),
+        )
+        quantise_labels(2)
+
+        like(1, 1)
+        weave_like(0, 2)
+        quantise_like(0, 1)
+        quantise_labels(3)
+        like(0, 3)
+        weave_like(1, 0)
+        quantise_like(0, 2)
+        like(1, 2)
+        weave_like(0, 3)
+        quantise_like(1, 0)
+        quantise_like(0, 3)
+        like(1, 3)
+        weave_like(1, 1)
+        weave_like(1, 2)
+        quantise_like(1, 1)
+
+        early, last = (0, 1, 2), (3,)
+        output_passes(0, early)
+        output_passes(1, early)
+        output_passes(0, last)
+        weave_like(1, 3, 0, SPAN // 2, nc.scalar.copy)
+        output_passes(1, last)
+        quantise_like(1, 2)
+        weave_like(1, 3, SPAN // 2, SPAN)
+        quantise_like(1, 3, 0, SPAN // 2)
+        quantise_like(1, 3, SPAN // 2, SPAN)
+        output_passes(2, early + last)
+        output_passes(3, early + last)
+        output_passes(4, early)
+        output_passes(5, early)
+        output_passes(4, last)
+        output_passes(5, last, copy=nc.vector.tensor_copy)
+        output_passes(6, early + last)
+        output_passes(7, early + last, 0, B // 2)
+        output_passes(7, early + last, B // 2, B, nc.vector.tensor_copy)

from contextlib import ExitStack

import concourse.mybir as mybir
from concourse.masks import make_identity

M, D, NPTS, R, B = 1024, 1024, 2048, 1024, 512
FLOPS = 2 * M * D * NPTS + 2 * R * NPTS * B + 2 * M * NPTS * B

F32 = mybir.dt.float32
BF16 = mybir.dt.bfloat16
I32 = mybir.dt.int32
U32 = mybir.dt.uint32
U8 = mybir.dt.uint8
FP8X4 = mybir.dt.float8_e4m3fn_x4
FP4X4 = mybir.dt.float4_e2m1fn_x4
ALU = mybir.AluOpType
ACT = mybir.ActivationFunctionType

P = 128
SPAN = 512
SLOTS = 4
BANKS = 8
RAW_BUFS = 8
SORTED_BUFS = 4
TURNED_BUFS = 3
ROWS_BUFS = 6
WOVEN_BUFS = 3
RESULT_BUFS = 6
WARM_BEFORE, WARM_AFTER = 3, 5


def tile_soft_demapper_label_sums_s12_kernel(
    tc, y, points, energy, prior, u_words, u_scales, v_words, v_scales, out
):
    nc = tc.nc
    with ExitStack() as ctx:
        keep = ctx.enter_context(tc.tile_pool(name="keep", bufs=1))
        work = ctx.enter_context(tc.tile_pool(name="work", bufs=WOVEN_BUFS))
        psum = ctx.enter_context(tc.psum_pool(name="psum", bufs=1))
        ctx.enter_context(tc.manual_schedule())

        def kept(name, shape, dtype):
            return keep.tile(shape, dtype, name=name, align_bytes=64)

        def streamed(name, shape, dtype, bufs):
            return work.tile(shape, dtype, name=name, tag=name, bufs=bufs, align_bytes=64)

        banks = []

        def new_bank():
            bank = psum.tile([P, SPAN], F32, name="bank%d" % len(banks), tag="bank%d" % (len(banks) % BANKS))
            banks.append(bank)
            return bank

        def mx_tiles(name, width):
            return kept(name + "_codes", [P, width], U32), kept(name + "_scales", [P, width], U8)

        def quantise(operand, values):
            nc.vector.quantize_mx(out=operand[0].bitcast(FP8X4), scales=operand[1], in_=values)

        def mx_pass(dst, lhs, rhs, dtype, first, last):
            nc.tensor.matmul_mx(
                out=dst,
                lhsT=lhs[0].bitcast(dtype),
                lhsT_scale=lhs[1],
                rhs=rhs[0].bitcast(dtype),
                rhs_scale=rhs[1],
                start=first,
                stop=last,
            )

        def columns(operand, lo, hi):
            return operand[0][:, lo:hi], operand[1][:, lo:hi]

        u_scale_rows = [kept("u_scale_rows%d" % k, [P, 2 * 2 * SPAN], U8) for k in range(2)]
        v_scale_rows = kept("v_scale_rows", [P, 2 * B], U8)
        nc.vector.memset(u_scale_rows[0][:].bitcast(I32), 0)
        nc.vector.memset(v_scale_rows[:].bitcast(I32), 0)
        probe = kept("probe", [P, 2], F32)
        nc.vector.memset(probe[:, 0:1], 1.0)
        nc.scalar.activation(out=probe[:, 1:2], in_=probe[:, 0:1], func=ACT.Ln)
        ident = kept("ident", [P, P], F32)
        make_identity(nc, ident[:])
        const_rows = kept("const_rows", [P, SPAN], F32)
        nc.gpsimd.memset(const_rows[:], 0.0)
        warm_values = kept("warm_values", [P, SLOTS * 2 * P], BF16)
        nc.vector.memset(warm_values[:].bitcast(I32), 0)
        nc.vector.memset(u_scale_rows[1][:].bitcast(I32), 0)
        warm = mx_tiles("warm", 2 * P)
        quantise(columns(warm, 0, 2 * P), warm_values[:])

        raw = {}
        u_raw = {}

        def load_rows(tile, half):
            src = y if tile[0] == "y" else points
            row0 = SPAN * tile[1] + 2 * P * half
            raw[tile, half] = streamed("raw", [P, 2, D], BF16, RAW_BUFS)
            nc.sync.dma_start(out=raw[tile, half][:], in_=src[row0 : row0 + 2 * P, :].rearrange("(a p) d -> p a d", p=P))

        def load_u(G):
            u_raw[G] = kept("u_raw%d" % G, [P, 2, 256], I32)
            words = u_words.bitcast(I32).rearrange("g p w -> p g w")
            nc.sync.dma_start(out=u_raw[G][:], in_=words[:, :, 256 * G : 256 * (G + 1)])

        def load_scales(plane, src):
            rows = src.bitcast(I32).rearrange("g (quad r) w -> r quad g w", r=4)
            for r in range(4):
                nc.sync.dma_start(out=plane[r:P:32, :].bitcast(I32).rearrange("p (g w) -> p g w", g=2), in_=rows[r])

        const_raw = kept("const_raw", [8, SPAN], BF16)
        nc.sync.dma_start(out=const_raw[4:8, :], in_=prior.rearrange("(g c) -> g c", g=4))
        nc.sync.dma_start(out=const_raw[0:4, :], in_=energy.rearrange("(g c) -> g c", g=4))
        load_u(0)
        v_codes = kept("v_codes", [P, 2 * 2 * B], U8)
        nc.sync.dma_start(
            out=v_codes[:].bitcast(I32).rearrange("p (g w) -> p g w", g=2),
            in_=v_words.bitcast(I32).rearrange("g p w -> p g w"),
        )
        load_scales(u_scale_rows[0], u_scales[:, :, 0 : 2 * SPAN])
        load_scales(v_scale_rows, v_scales)
        load_rows(("y", 0), 0)
        load_rows(("y", 0), 1)
        load_u(1)
        load_rows(("x", 0), 0)
        load_rows(("x", 0), 1)
        load_rows(("x", 1), 0)
        load_scales(u_scale_rows[1], u_scales[:, :, 2 * SPAN : 4 * SPAN])
        load_u(2)
        load_rows(("x", 1), 1)
        load_rows(("x", 2), 0)
        load_rows(("x", 2), 1)
        load_u(3)

        sorted_rows = {}
        turned = {}
        rows_mx = {}

        def sort_rows(tile, half, copy=nc.vector.tensor_copy):
            dst = streamed("sorted_rows", [P, 2, D], BF16, SORTED_BUFS)
            copy(
                out=dst[:].rearrange("p u (b e) -> p u b e", e=16),
                in_=raw[tile, half][:].rearrange("p a (b u e) -> p u (a b) e", u=2, e=16),
            )
            sorted_rows[tile, half] = dst

        def turn(tile):
            turned[tile] = streamed("turned", [P, 2 * SLOTS * SPAN], BF16, TURNED_BUFS)
            rows_mx[tile] = mx_tiles("%s%d" % tile, 2 * SPAN)
            for half in range(2):
                words = sorted_rows[tile, half][:].bitcast(F32)
                for g in range(2):
                    bank = new_bank()
                    for u in range(2):
                        for a in range(2):
                            nc.tensor.transpose(
                                bank[:, 2 * P * u + P * a : 2 * P * u + P * (a + 1)],
                                words[:, u, 2 * P * a + P * g : 2 * P * a + P * (g + 1)],
                                ident[:],
                            )
                    dst = turned[tile][:, SLOTS * SPAN * g : SLOTS * SPAN * (g + 1)].bitcast(F32)
                    if tile[0] == "y":
                        nc.scalar.copy(
                            out=dst[:, SPAN * half : SPAN * (half + 1)].rearrange("p (n u) -> p n u", u=2),
                            in_=bank[:].rearrange("p (u n) -> p n u", u=2),
                        )
                    else:
                        nc.scalar.copy(
                            out=dst.rearrange("p (t h q r u) -> p h t q r u", t=4, h=2, r=8, u=2)[:, half],
                            in_=bank[:].rearrange("p (u q t r) -> p t q r u", u=2, t=4, r=8),
                        )

        def quantise_rows(tile):
            quantise(columns(rows_mx[tile], 0, 2 * SPAN), turned[tile][:])

        consts = kept("consts", [P, 8, SLOTS], F32)
        energy_cols = consts[:, 0:4, :].rearrange("p g t -> p (g t)")
        prior_cols = consts[:, 4:8, :].rearrange("p g t -> p (g t)")
        magnitude = kept("magnitude", [P, 16], F32)
        twice_positive = kept("twice_positive", [P, 16], F32)
        sign = kept("sign", [P, 16], F32)
        factors = kept("factors", [P, 3, 16], F32)
        logs = kept("logs", [P, 3, 16], F32)
        log_prior = kept("log_prior", [P, 16], F32)
        bias = kept("bias", [P, 16], F32)

        def sort_consts():
            nc.vector.tensor_copy(
                out=const_rows[0:8, :].rearrange("p (t q r) -> p t q r", t=4, r=8),
                in_=const_raw[:].rearrange("p (q t r) -> p t q r", t=4, r=8),
            )

        def turn_consts():
            bank = new_bank()
            for t in range(SLOTS):
                nc.tensor.transpose(bank[:, P * t : P * (t + 1)], const_rows[:, P * t : P * (t + 1)], ident[:])
            nc.scalar.copy(out=consts[:], in_=bank[:].rearrange("p (t c) -> p c t", t=4)[:, 0:8, :])

        def sign_and_logs():
            nc.vector.scalar_tensor_tensor(
                out=magnitude[:], in0=prior_cols, scalar=-1.0, in1=prior_cols, op0=ALU.mult, op1=ALU.max
            )
            nc.vector.tensor_scalar(
                out=twice_positive[:], in0=prior_cols, scalar1=0.0, scalar2=2.0, op0=ALU.is_ge, op1=ALU.mult
            )
            for k, (s1, s2, op0, op1) in enumerate(
                (
                    (2.0**-63, 2.0**64, ALU.max, ALU.min),
                    (2.0**-126, 2.0**-63, ALU.max, ALU.min),
                    (2.0**-64, 1.0, ALU.mult, ALU.max),
                )
            ):
                nc.vector.tensor_scalar(out=factors[:, k, :], in0=magnitude[:], scalar1=s1, scalar2=s2, op0=op0, op1=op1)
            nc.vector.tensor_scalar(out=sign[:], in0=twice_positive[:], scalar1=-1.0, scalar2=None, op0=ALU.add)
            nc.scalar.activation(out=logs[:, 1, :], in_=factors[:, 1, :], func=ACT.Ln, scale=2.0**63)
            nc.scalar.activation(out=logs[:, 0:3:2, :], in_=factors[:, 0:3:2, :], func=ACT.Ln)

        def sum_logs():
            nc.vector.tensor_reduce(
                out=log_prior[:], in_=logs[:].rearrange("p s c -> p c s"), axis=mybir.AxisListType.X, op=ALU.add
            )

        def make_bias():
            nc.vector.tensor_tensor(out=bias[:], in0=log_prior[:], in1=energy_cols, op=ALU.subtract)

        def weave(dst, rows, lo, hi, copy=nc.vector.tensor_copy):
            copy(
                out=dst[:, SLOTS * lo : SLOTS * hi].rearrange("p (c i t) -> p c t i", i=4, t=4),
                in_=rows[:, :, lo:hi].rearrange("p t (c i) -> p c t i", i=4),
            )

        u_codes = {}
        u_planes = {}
        label_banks = {}
        label_rows = {}
        label_woven = {}
        label_mx = {}

        def sort_u_codes(G):
            u_codes[G] = kept("u_codes%d" % G, [P, 2 * 2 * SPAN], U8)
            nc.vector.tensor_copy(
                out=u_codes[G][:].bitcast(I32).rearrange("p (g t q w) -> p g t q w", g=2, t=4, w=4),
                in_=u_raw[G][:].rearrange("p g (q t w) -> p g t q w", t=4, w=4),
            )

        def sort_u_scales(G):
            u_planes[G] = kept("u_plane%d" % G, [P, 2 * SPAN], U8)
            both = u_scale_rows[G // 2][:].bitcast(I32).rearrange("p (g k q t w) -> p k g t q w", g=2, q=16, t=4, w=2)
            nc.vector.tensor_copy(
                out=u_planes[G][:].bitcast(I32).rearrange("p (g t q w) -> p g t q w", g=2, t=4, w=2),
                in_=both[:, G % 2],
            )

        def u_operand(G, g, t):
            lo = SPAN * g + P * t
            return u_codes[G][:, 2 * lo : 2 * (lo + P)], u_planes[G][:, lo : lo + P]

        def v_operand(g, lo, hi):
            return v_codes[:, 2 * (B * g + lo) : 2 * (B * g + hi)], v_scale_rows[:, B * g + lo : B * g + hi]

        def labels_wide(G, t):
            if t == 0:
                label_rows[G] = streamed("rows", [P, SLOTS, SPAN], BF16, ROWS_BUFS)
            bank = new_bank()
            for g in range(2):
                mx_pass(bank[:], u_operand(G, g, t), v_operand(g, 0, B), FP4X4, g == 0, g == 1)
            col = SLOTS * G + t
            nc.scalar.activation(out=label_rows[G][:, t, :], in_=bank[:], func=ACT.Copy, scale=sign[:, col : col + 1])

        def weave_labels(G):
            label_woven[G] = streamed("label_woven", [P, SLOTS * B], BF16, WOVEN_BUFS)
            weave(label_woven[G], label_rows[G], 0, B)

        def labels_narrow(G, c):
            if c == 0:
                label_woven[G] = streamed("label_woven", [P, SLOTS * B], BF16, WOVEN_BUFS)
            bank = new_bank()
            for t in range(SLOTS):
                for g in range(2):
                    mx_pass(
                        bank[:, P * t : P * (t + 1)], u_operand(G, g, t), v_operand(g, P * c, P * (c + 1)), FP4X4, g == 0, g == 1
                    )
            label_banks[G, c] = bank

        def empty_labels(G, c):
            nc.vector.tensor_tensor(
                out=label_woven[G][:, SPAN * c : SPAN * (c + 1)].rearrange("p (n t) -> p n t", t=4),
                in0=label_banks[G, c][:].rearrange("p (t n) -> p n t", t=4),
                in1=sign[:, SLOTS * G : SLOTS * (G + 1)].unsqueeze(1).to_broadcast([P, P, SLOTS]),
                op=ALU.mult,
            )

        def quantise_labels(G):
            label_mx[G] = mx_tiles("label%d" % G, B)
            quantise(columns(label_mx[G], 0, B), label_woven[G][:])

        like_rows = {}
        like_woven = {}
        like_mx = {}

        def like(h, G):
            like_rows[h, G] = streamed("rows", [P, SLOTS, SPAN], BF16, ROWS_BUFS)
            like_mx[h, G] = mx_tiles("like%d%d" % (h, G), SPAN)
            for t in range(SLOTS):
                bank = new_bank()
                for g in range(2):
                    lhs = columns(rows_mx["x", G], SPAN * g + P * t, SPAN * g + P * (t + 1))
                    rhs = columns(rows_mx["y", h], SPAN * g, SPAN * (g + 1))
                    mx_pass(bank[:], lhs, rhs, FP8X4, g == 0, g == 1)
                col = SLOTS * G + t
                nc.scalar.activation(out=like_rows[h, G][:, t, :], in_=bank[:], func=ACT.Exp, bias=bias[:, col : col + 1])

        def weave_like(h, G, lo=0, hi=SPAN, copy=nc.vector.tensor_copy):
            if lo == 0:
                like_woven[h, G] = streamed("like_woven", [P, SLOTS * SPAN], BF16, WOVEN_BUFS)
            weave(like_woven[h, G], like_rows[h, G], lo, hi, copy)

        def quantise_like(h, G, lo=0, hi=SPAN):
            quantise(columns(like_mx[h, G], lo, hi), like_woven[h, G][:, SLOTS * lo : SLOTS * hi])

        sums = {}

        def output_passes(i, groups, lo=0, hi=B, copy=nc.scalar.copy):
            if groups[0] == 0:
                sums[i] = new_bank()
            for G in groups:
                lhs = columns(like_mx[i // 4, G], P * (i % 4), P * (i % 4 + 1))
                mx_pass(sums[i][:, lo:hi], lhs, columns(label_mx[G], lo, hi), FP8X4, G == 0, G == 3)
            if groups[-1] == 3:
                result = streamed("result", [P, B], F32, RESULT_BUFS)
                copy(out=result[:, lo:hi], in_=sums[i][:, lo:hi])
                nc.sync.dma_start(out=out[P * i : P * (i + 1), lo:hi], in_=result[:, lo:hi])

        def warm_up(passes):
            bank = new_bank()
            for k in range(passes):
                mx_pass(bank[:, 0 : 2 * P], columns(warm, 0, P), columns(warm, 0, 2 * P), FP8X4, True, True)


        warm_up(WARM_BEFORE)
        sort_consts()
        sort_u_codes(0)
        turn_consts()
        sort_u_scales(0)
        warm_up(WARM_AFTER)
        sign_and_logs()
        for half in range(2):
            labels_wide(0, 2 * half)
            labels_wide(0, 2 * half + 1)
            sort_rows(("y", 0), half)
        sort_u_scales(1)
        sort_u_codes(1)

        turn(("y", 0))
        nc.scalar.activation(out=probe[:, 1:2], in_=logs[:, 1, 0:1], func=ACT.Exp)
        sum_logs()
        load_rows(("y", 1), 0)
        load_rows(("y", 1), 1)
        labels_narrow(1, 0)
        sort_rows(("x", 0), 0)
        labels_narrow(1, 1)
        empty_labels(1, 0)
        sort_rows(("x", 0), 1)
        load_rows(("x", 3), 0)
        load_rows(("x", 3), 1)
        labels_narrow(1, 2)
        labels_narrow(1, 3)
        quantise_rows(("y", 0))
        sort_u_codes(2)
        sort_u_scales(2)

        turn(("x", 0))
        empty_labels(1, 1)
        sort_rows(("x", 1), 0)
        empty_labels(1, 2)
        labels_narrow(2, 0)
        labels_narrow(2, 1)
        empty_labels(1, 3)
        sort_rows(("x", 1), 1, nc.scalar.copy)
        labels_narrow(2, 2)
        make_bias()
        quantise_rows(("x", 0))

        def one_round(tile, following, group, full_banks, new_banks, before, after):
            turn(tile)
            for bank_key in full_banks:
                empty_labels(*bank_key)
            for half in range(2 if following else 0):
                sort_rows(following, half)
            like(*group)
            before()
            for bank_key in new_banks:
                labels_narrow(*bank_key)
            quantise_rows(tile)
            after()

        one_round(
            ("x", 1), ("x", 2), (0, 0), [(2, 0), (2, 1), (2, 2)], [(2, 3)],
            lambda: sort_u_codes(3), lambda: sort_u_scales(3),
        )
        one_round(
            ("x", 2), ("y", 1), (0, 1), [(2, 3)], [(3, 0), (3, 1)],
            lambda: weave_like(0, 0), lambda: quantise_labels(1),
        )
        one_round(
            ("y", 1), ("x", 3), (0, 2), [(3, 0), (3, 1)], [(3, 2), (3, 3)],
            lambda: weave_labels(0), lambda: quantise_like(0, 0),
        )
        one_round(
            ("x", 3), None, (1, 0), [(3, 2), (3, 3)], [],
            lambda: weave_like(0, 1), lambda: quantise_labels(0),
        )
        quantise_labels(2)

        like(1, 1)
        weave_like(0, 2)
        quantise_like(0, 1)
        quantise_labels(3)
        like(0, 3)
        weave_like(1, 0)
        quantise_like(0, 2)
        like(1, 2)
        weave_like(0, 3)
        quantise_like(1, 0)
        quantise_like(0, 3)
        like(1, 3)
        weave_like(1, 1)
        weave_like(1, 2)
        quantise_like(1, 1)

        early, last = (0, 1, 2), (3,)
        output_passes(0, early)
        output_passes(1, early)
        output_passes(0, last)
        weave_like(1, 3, 0, SPAN // 2, nc.scalar.copy)
        output_passes(1, last)
        quantise_like(1, 2)
        weave_like(1, 3, SPAN // 2, SPAN)
        quantise_like(1, 3, 0, SPAN // 2)
        quantise_like(1, 3, SPAN // 2, SPAN)
        output_passes(2, early + last)
        output_passes(3, early + last)
        output_passes(4, early)
        output_passes(5, early)
        output_passes(4, last)
        output_passes(5, last, copy=nc.vector.tensor_copy)
        output_passes(6, early + last)
        output_passes(7, early + last, 0, B // 2)
        output_passes(7, early + last, B // 2, B, nc.vector.tensor_copy)
